import numpy as np, ml_dtypes
CORES = [1,5,17,21,33,37,49,53]
N = 8
BF = ml_dtypes.bfloat16
def gentries(a):
    return np.ascontiguousarray(a.reshape(8, 16, -1).transpose(0, 2, 1)).reshape(8, -1)
def gtable(e):
    e = np.asarray(e); return np.ascontiguousarray(e.reshape(8, -1, 16).transpose(0, 2, 1)).reshape(128, -1).astype(np.int32)
W, V, Q, L, B, RO = 2816, 1280, 5, 256, 4, 6
def parts(rng):
    x = rng.integers(0, 16, (N, 8, 16, W)); s = rng.integers(0, 256, (N, 8, 16, W))
    p = rng.integers(0, W, (N, 8, 16, V)); u = rng.integers(0, V, (N, 8, 16, V))
    share = rng.choice(np.array([0.0006, 0.0025, 0.008, 0.025]), (N, 8, 1, 1))
    m = np.where(rng.random((N, 8, 16, V)) < share, rng.integers(8, 16, (N, 8, 16, V)), rng.integers(0, 8, (N, 8, 16, V)))
    h = np.ascontiguousarray(np.argsort(rng.random((N, 8, V)), axis=-1)[..., :B * L])
    c = rng.integers(132, 157, (N, 8, 1)) + rng.integers(0, 8, (N, 8, 16)); t = rng.integers(45, 111, (N, 8, 16, RO))
    return x, s, p, u, m, h, c, t
def pack(x, s, p, u, m, h, c, t):
    def w(a): return np.ascontiguousarray(a.reshape(N, 128, -1))
    return {"xf": w(x).astype(np.float32).astype(BF), "stp": w(s).astype(np.float32).astype(BF), "pl": w(p).astype(np.int32), "su": w(u).astype(np.int32),
            "mk": w(m).astype(np.float32).astype(BF), "hp": np.stack([gtable(a) for a in h]), "cp": w(c).astype(np.int32), "th": w(t).astype(np.int32)}
def setup_inputs(rng):
    return pack(*parts(rng))
def uneven(rng, n, k, e):
    return np.minimum((n * rng.random((N, 8, 16, k)) ** np.exp2(e)).astype(np.int64), n - 1)
def setup_inputs_spread(rng):
    x, s, p, u, m, h, c, t = parts(rng)
    x = uneven(rng, 16, W, rng.integers(-2, 3, (N, 8, 1, W))); s = uneven(rng, 256, W, rng.integers(-2, 3, (N, 8, 1, W)))
    p = uneven(rng, W, V, rng.integers(-2, 3, (N, 8, 1, 1))); u = uneven(rng, V, V, rng.integers(-2, 3, (N, 8, 1, 1)))
    m = np.where(rng.random((N, 8, 16, V)) < rng.choice(np.array([0.0, 0.0, 0.0, 0.0, 0.01, 0.05]), (N, 8, 1, V)), rng.integers(0, 16, (N, 8, 16, V)), 0)
    c = rng.integers(0, 241, (N, 8, 16)); t = rng.integers(1, 241, (N, 8, 16, RO))
    c[:, 1::2] = rng.integers(100, 241, (N, 4, 16)); t[:, 1::2] = rng.integers(100, 241, (N, 4, 16, RO))
    return pack(x, s, p, u, m, h, c, t)
def binary(rng, n):
    k = rng.integers(0, 3, (N, 8, 1, n)); return np.where(k == 2, rng.integers(0, 2, (N, 8, 16, n)), k)
def setup_inputs_ends(rng):
    x, s, p, u, m, h, c, t = parts(rng)
    x = 15 * binary(rng, W); s = 255 * binary(rng, W)
    x[..., 0] = 0; x[..., 1] = 15; x[..., 2] = 15; x[..., W - 1] = 15; x[:, 1:6:2, :, 0] = 15 * rng.integers(0, 2, (N, 3, 16))
    s[..., W - 1] = 255 * rng.integers(0, 2, (N, 8, 16)); s[..., 0] = 255 * rng.integers(0, 2, (N, 8, 16))
    k = rng.integers(0, 10, (N, 8, 1, V)); z = rng.random((N, 8, 16, V))
    p = np.where(k < 2, 0, np.where(k < 4, W - 1, np.where(z < 0.35, 0, np.where(z < 0.7, W - 1, p))))
    p[..., 0] = 0; p[..., V - Q:] = W - 1
    k = rng.integers(0, 10, (N, 8, 1, V)); z = rng.random((N, 8, 16, V))
    u = np.where(k < 4, 0, np.where(k < 6, V - 1, np.where(z < 0.25, 0, np.where(z < 0.5, V - 1, u))))
    m = 15 * ((rng.random((N, 8, 1, V)) < 0.03) | (rng.random((N, 8, 16, V)) < 0.004)).astype(np.int64)
    m[..., 0] = 0; m[..., V - 1] = 15 * rng.integers(0, 2, (N, 8, 16)); m[N - 1, 7, :, V - 1] = 15
    e = np.stack([np.arange(V // 2), V - 1 - np.arange(V // 2)], axis=1).reshape(-1)[:B * L]
    h[:, (0, 2, 6)] = e; h[:, (1, 3, 7)] = e[::-1]
    k = np.stack([rng.permutation(np.array([0, 0, 0, 1, 1, 2, 2, 2])) for r in range(N)])[:, :, None]
    c = 240 * np.where(k == 2, rng.integers(0, 2, (N, 8, 16)), k); c[N - 1, 7] = 0
    t = np.where(rng.random((N, 8, 16, RO)) < 0.25, 1, 240)
    return pack(x, s, p, u, m, h, c, t)
def setup_inputs_corners(rng):
    x, s, p, u, m, h, c, t = parts(rng)
    near = rng.random((N, 8, 16, V)) < 0.25; p = np.where(near, W - 1 - rng.integers(0, 256, (N, 8, 16, V)), p)
    a = W - np.arange(W - 255, W); s[..., W - 255:] = np.minimum(a + rng.integers(-1, 2, (N, 8, 16, 255)), 255)
    x[:, ::2] = 7 + (np.arange(W) & 1)
    odd = (rng.random((N, 4, 16, V)) < rng.random((N, 4, 1, V))).astype(np.int64); p[:, ::2] = (p[:, ::2] >> 1) * 2 + odd
    c[:, ::2] = 112 + rng.integers(4, 13, (N, 4, 16)); t[:, ::2] = rng.integers(7, 9, (N, 4, 16, RO)) * rng.integers(6, 17, (N, 4, 16, RO)) + rng.integers(0, 2, (N, 4, 16, RO))
    m = rng.choice(np.array([0, 3, 4, 7, 8, 11, 12, 15]), (N, 8, 16, V), p=np.array([0.3, 0.15, 0.15, 0.308, 0.04, 0.05, 0.001, 0.001]))
    v = np.arange(V)
    for r in range(N):
        o = rng.permutation(8)
        m[r, o[0]] = 15; m[r, o[1]] = 0
        m[r, o[2]] = np.where(rng.random((16, V)) < 0.002, rng.integers(11, 13, (16, V)), 7)
        o = rng.permutation(8)
        u[r, o[0]] = v; u[r, o[1]] = (v + V - 1) % V; u[r, o[2]] = rng.choice(np.array([0, V - 1]), (16, V)); u[r, o[3]] = (v + 1) % V
        p[r, o[4]] = p[r, o[4], :1]
    return pack(x, s, p, u, m, h, c, t)
def setup_inputs_crowd(rng):
    x, s, p, u, m, h, c, t = parts(rng)
    for r in range(N):
        o = rng.permutation(8)
        for i in range(6):
            g = o[i]; lone = Q * int(rng.choice(np.array([0, L // 2, L - 1]))) + np.arange(Q)
            w = rng.permutation(np.setdiff1d(np.arange(V), lone)); hot = w[:16]
            m[r, g] = 0
            if i < 4: c[r, g] = 240
            if i in (0, 1, 3): m[r, g, np.arange(16), hot] = 15
            if i < 2: u[r, g] = hot[:, None]
            if i == 1: u[r, g][:, lone] = lone
            if i == 2: u[r, g] = V - 1
            if i == 3: u[r, g] = w[16]; u[r, g][:, lone] = hot[:, None]
            if i >= 4:
                p[r, g] = W - 1; x[r, g, :, W - 1] = 15; x[r, g, :, 0] = 0
                c[r, g] = rng.integers(229, 237, 16); t[r, g] = rng.integers(1, 121, (16, RO)); u[r, g] = V - 1
            if i == 5: p[r, g][:, lone] = 0; u[r, g] = np.arange(V)
    return pack(x, s, p, u, m, h, c, t)
def setup_inputs_tides(rng):
    x, s, p, u, m, h, c, t = parts(rng); x = np.minimum(x, 14); q = rng.permutation(N); a, b, e = int(q[0]), int(q[1]), int(q[2]); v = np.arange(V)
    for g in range(8):
        o = rng.permutation(16)[:RO]
        m[:, g, o] = m[:, g, o] & 7; t[:, g, o] = 240
        for r in (a, e):
            m[r, g] = m[r, g] & 7; u[r, g] = Q * rng.integers(0, L, (16, V)) + v % Q
        x[a, g] = np.maximum(x[a, g], 1); c[a, g, ::2] = rng.integers(0, 9, 8); t[a, g, o, np.arange(RO)] = rng.integers(1, 9, RO)
        k = rng.integers(0, 12, (16, V)); k[o] = k[o] & 7; m[b, g] = k
        c[b, g] = 240; t[b, g] = rng.integers(1, 241, (16, RO))
        c[e, g] = rng.integers(116, 141, 16); t[e, g] = 240
        even = np.arange(0, RO, 2); t[e, g, o[even], even] = rng.integers(24, 57, len(even))
    return pack(x, s, p, u, m, h, c, t)
def check_inputs(d):
    bad = []
    for k, lo, hi in (("xf", 0, 15), ("stp", 0, 255), ("pl", 0, W - 1), ("su", 0, V - 1), ("mk", 0, 15), ("hp", 0, V - 1), ("cp", 0, 240), ("th", 1, 240)):
        v = np.asarray(d[k]).astype(np.float64)
        if not np.all((v >= lo) & (v <= hi)): bad.append("range of " + k)
        elif not np.all(v == np.floor(v)): bad.append("whole numbers in " + k)
    e = np.sort(np.stack([gentries(a) for a in d["hp"]]), axis=-1)
    if np.any(e[..., 1:] == e[..., :-1]): bad.append("repeats in hp")
    return bad
def pick(a, ix):
    return np.stack([np.stack([np.take(a[r, g], ix[r, g], axis=1) for g in range(8)]) for r in range(N)])
def reference(xf, stp, pl, su, mk, hp, cp, th):
    x = xf.astype(np.float32).astype(np.int32).reshape(N, 8, 16, W); s = stp.astype(np.float32).astype(np.int32).reshape(N, 8, 16, W)
    p = pl.astype(np.int32).reshape(N, 8, 16, V); nx = su.astype(np.int32).reshape(N, 8, 16, V); m = mk.astype(np.float32).astype(np.int32).reshape(N, 8, 16, V)
    h = np.stack([gentries(a) for a in hp]).astype(np.int32).reshape(N, 8, B, L); cap = cp.astype(np.int32).reshape(N, 8, 16, 1); theta = th.astype(np.int32).reshape(N, 8, 16, RO)
    wt = (2 * np.arange(16, dtype=np.int32) + 1).reshape(1, 1, 16, 1); A = np.zeros((N, 8, 1, 1), np.int32)
    for t in range(RO):
        lanes = slice(t % Q, V, Q)
        old = m[..., lanes].copy(); at = p[..., lanes].copy()
        climb = np.max(pick(m, nx[..., lanes].reshape(N, 8, 16 * L)).reshape(N, 8, 16, 16, L), axis=3)
        new = np.maximum(old, climb - 4)
        ix = at.reshape(N, 8, 16 * L)
        xk = pick(x, ix).reshape(N, 8, 16, 16, L)
        S = np.add.reduce(xk, axis=3)
        over = S > cap + (A & 7)
        load = np.add.reduce(np.where(over[:, :, :, None, :], xk, 0), axis=2)
        new = np.where(load >= theta[..., t:t + 1], 15, new)
        opened = np.any((new >= 8) & (old < 8), axis=2)
        u = np.add.reduce(wt * S, axis=2)
        move = np.where(new >= 8, np.maximum(u & 15, 1)[:, :, None, :], 0)
        sk = pick(s, ix).reshape(N, 8, 16, 16, L)
        child = at + np.take_along_axis(sk, move[:, :, None], axis=2)[:, :, 0]
        child = np.where(child >= W, child - W, child)
        c = np.take_along_axis(h, ((u >> 4) & (B - 1))[:, :, None], axis=2)[:, :, 0]
        A = np.add.reduce(opened.astype(np.int32), axis=2).reshape(N, 8, 1, 1)
        m[..., lanes] = new
        back = np.zeros((N, 8, 16, L), np.int32)
        for r in range(N):
            d = (r + 1 + t % (N - 1)) % N
            for g in range(8):
                i = np.flatnonzero(opened[r, g]); cc = c[r, g, i]
                back[r, g][:, i] = m[d, g][:, cc]
                p[d, g][:, cc] = child[r, g][:, i]; m[d, g][:, cc] = 0
        now = m[..., lanes]
        m[..., lanes] = np.where(opened[:, :, None, :], np.maximum(now, back - 4), now)
    return {"ypl": p.reshape(N, 128, V).astype(np.float32), "ymk": m.reshape(N, 128, V).astype(np.float32).astype(BF)}

@@ -1,0 +1,466 @@
+from concourse.bass import DstId, RemoteDMATransfer
+from concourse.mybir import dt, AluOpType, AxisListType, ActivationFunctionType
+
+W, V, Q, L, RO = 2816, 1280, 5, 256, 6
+H = 4096
+N1 = 2
+BIG = 16384.0
+
+F32, BF, F16, I32, U16 = "float32", "bfloat16", "float16", "int32", "uint16"
+SCRATCH = {
+    "XT": ("sbuf", [128, 2 * H], BF), "ST": ("sbuf", [128, 2 * H], BF),
+    "XK": ("sbuf", [128, 4096], BF), "SK": ("sbuf", [128, 4096], BF), "TR": ("sbuf", [128, 4096], BF),
+    "PR": ("sbuf", [128, 2048], F16),
+    "pp": ("sbuf", [128, V + L], F32), "mm": ("sbuf", [128, V + L], F32),
+    "PL": ("sbuf", [128, V], I32), "SU": ("sbuf", [128, V], I32), "MK": ("sbuf", [128, V], BF),
+    "OFF": ("sbuf", [128, V], U16), "LST": ("sbuf", [128, L], U16), "LS0": ("sbuf", [128, L], U16),
+    "ZA": ("sbuf", [128, 2048], BF), "Z": ("sbuf", [128, 2048], BF), "Z2": ("sbuf", [128, 2048], BF), "ZM": ("sbuf", [128, 2048], BF),
+    "GE8": ("sbuf", [128, L], BF), "NEWA": ("sbuf", [128, L], BF), "HI": ("sbuf", [128, L], BF),
+    "OV": ("sbuf", [128, L], BF), "SB": ("sbuf", [128, L], BF), "SJ": ("sbuf", [128, L], BF), "HD": ("sbuf", [128, L], BF),
+    "JK": ("sbuf", [128, L], BF), "NEG": ("sbuf", [128, L], F32),
+    "TI": ("sbuf", [128, L], I32), "LI": ("sbuf", [128, L], I32),
+    "WF": ("sbuf", [128, L], F32), "WY": ("sbuf", [128, L], F32), "FL": ("sbuf", [128, V], BF),
+    "HP": ("sbuf", [128, 64], I32), "HF": ("sbuf", [128, 64], F32), "D1": ("sbuf", [128, 48], F32), "D2": ("sbuf", [128, 32], F32),
+    "KC": ("sbuf", [128, 64], F32), "D0": ("sbuf", [128, 64], F32), "C6": ("sbuf", [128, 64], F32),
+    "CP": ("sbuf", [128, 1], I32), "TH": ("sbuf", [128, RO], I32), "THF": ("sbuf", [128, RO], F32),
+    "CAPB": ("sbuf", [128, 1], F32), "BIAS": ("sbuf", [128, 1], F32), "AC": ("sbuf", [128, 1], F32),
+    "AI": ("sbuf", [128, 1], I32), "A7": ("sbuf", [128, 1], I32),
+    "U": ("sbuf", [128, 32], I32), "BB": ("sbuf", [128, 16], I32), "J1": ("sbuf", [128, 16], I32),
+    "J2": ("sbuf", [128, 16], F32), "J3": ("sbuf", [128, 16], F32), "JL": ("sbuf", [128, 16], U16), "L6": ("sbuf", [128, 16], F32),
+    "PID": ("sbuf", [128, 1], I32), "CI": ("sbuf", [128, 8], I32), "CF": ("sbuf", [128, 16], F32),
+    "NR": ("sbuf", [128, 160], F32), "G16R": ("sbuf", [128, 128], F32), "PARW": ("sbuf", [128, 128], F32),
+    "WN": ("sbuf", [128, 160], BF), "WS": ("sbuf", [128, 160], BF), "BP": ("sbuf", [128, 160], BF), "BN": ("sbuf", [128, 160], BF),
+    "LW": ("sbuf", [128, 160], F16), "LA": ("sbuf", [128, 160], F32), "LB": ("sbuf", [128, 160], F32),
+    "I0P": ("sbuf", [128, 160], BF), "I1P": ("sbuf", [128, 160], BF), "I0N": ("sbuf", [128, 160], BF), "I1N": ("sbuf", [128, 160], BF),
+    "ID": ("sbuf", [128, 128], BF), "IDS": ("sbuf", [128, 128], BF), "ID32": ("sbuf", [128, 128], F32), "ID6": ("sbuf", [128, 128], F16),
+    "BOP": ("sbuf", [128, 128], BF), "BON": ("sbuf", [128, 128], BF), "BO1": ("sbuf", [128, 128], F32), "COR": ("sbuf", [128, 128], BF),
+    "JB": ("sbuf", [128, 16], F32), "DUM": ("sbuf", [128, 16], F16),
+    "cS": ("sbuf", [128, RO * 16], U16), "cR": ("sbuf", [128, RO * 16], U16),
+    "lS": ("sbuf", [128, RO * 16], U16), "lR": ("sbuf", [128, RO * 16], U16),
+    "bS": ("sbuf", [128, RO * L], BF), "bR": ("sbuf", [128, RO * L], BF),
+    "kS": ("sbuf", [128, RO * L], U16), "kR": ("sbuf", [128, RO * L], U16),
+}
+for _b in range(8):
+    SCRATCH["B%d" % _b] = ("psum", [128, 512], F32)
+
+DMAS = ["pl", "xf", "mk", "su", "st0", "st1", "sm", "ypl", "ymk"]
+SEMAPHORES = ["cV", "cA", "cP", "cG", "sent"] + ["d_" + n for n in DMAS] + \
+             ["r%s%d" % (k, t) for k in "clbk" for t in range(RO)]
+
+
+def rank_program(g, core, T, topo):
+    rank = T.rank_of(core)
+    if rank is None:
+        return
+    cores = T.cores
+    n = len(cores)
+    A_ = AluOpType
+    AF = ActivationFunctionType
+    Qs = {"V": g.vector, "A": g.scalar, "P": g.tensor, "G": g, "S": g.sync}
+    cnt = {"cV": 0, "cA": 0, "cP": 0, "cG": 0}
+    known = {q: {} for q in Qs}
+    lastw, readers, bank = {}, {}, {}
+    total = {}
+
+    def wait(q, toks):
+        need = {}
+        for tk in toks:
+            if known[q].get(tk[0], 0) < tk[1] and need.get(tk[0], (0, 0))[1] < tk[1]:
+                need[tk[0]] = tk
+        for s, tk in need.items():
+            if not any(o[0] != s and o[2].get(s, 0) >= tk[1] for o in need.values()):
+                Qs[q].wait_ge(T.sem[s], tk[1])
+        for tk in toks:
+            for s, v in list(tk[2].items()) + [(tk[0], tk[1])]:
+                if known[q].get(s, 0) < v:
+                    known[q][s] = v
+
+    def deps(q, r, w, b):
+        toks = []
+        for k in r:
+            if k in lastw: toks.append(lastw[k])
+        for k in w:
+            if k in lastw: toks.append(lastw[k])
+            toks.extend(readers.get(k, []))
+        for k in b:
+            toks.extend(tk for e, tk in bank.get(k, {}).items() if e != q)
+        if q == "P":
+            toks = [tk for tk in toks if tk[0] != "cP"]
+        return toks
+
+    def note(q, tok, r, w, b):
+        for k in r: readers.setdefault(k, []).append(tok)
+        for k in w:
+            lastw[k] = tok
+            readers[k] = []
+        for k in b: bank.setdefault(k, {})[q] = tok
+
+    def op(q, fn, r=(), w=(), b=(), sig=True):
+        wait(q, deps(q, r, w, b))
+        ins = fn()
+        s = "c" + q
+        if sig:
+            cnt[s] += 1
+            ins.then_inc(T.sem[s], 1)
+            total[s] = cnt[s]
+            tok = (s, cnt[s], dict(known[q]))
+        else:
+            tok = (s, cnt[s] + 1, dict(known[q]))
+        note(q, tok, r, w, b)
+
+    def dmas(name, items, r=(), w=()):
+        s = "d_" + name
+        kn = {}
+        for q, out, in_ in items:
+            wait(q, deps(q, r, w, ()))
+            Qs[q].dma_start(out, in_).then_inc(T.sem[s], 16)
+            kn = dict(known[q])
+        total[s] = 16 * len(items)
+        note("S", (s, total[s], kn), r, w, ())
+
+    neng = min(len(topo.engines(a, b)) for a in cores for b in cores if a != b)
+
+    def send(kind, t, dst, width):
+        key = "%sS%d" % (kind, t)
+        wait("G", deps("G", [key], (), ()))
+        rid, pid, _ = topo.addr(dst)
+        mask = sum(1 << e for e in topo.engines(core, dst)[:neng])
+        sl = slice(t * width, (t + 1) * width)
+        g.remote_dma(T[kind + "R"][:, sl], T[kind + "S"][:, sl], T.sem["r%s%d" % (kind, t)], T.sem.sent, pid, rid, mask)
+        total["sent"] = total.get("sent", 0) + neng
+
+    for kind in "clbk":
+        for t in range(RO):
+            s = "r%s%d" % (kind, t)
+            lastw["%sR%d" % (kind, t)] = (s, neng, {})
+            total[s] = neng
+
+    vec, act, pe = g.vector, g.scalar, g.tensor
+
+    def ts(out, in0, s1, s2, o0, o1, r, w, b=()):
+        if o1 is None:
+            op("V", lambda: vec.tensor_scalar(out, in0, s1, None, o0), r, w, b)
+        else:
+            op("V", lambda: vec.tensor_scalar(out, in0, s1, s2, o0, o1), r, w, b)
+
+    def tt(out, in0, in1, o, r, w, b=()):
+        op("V", lambda: vec.tensor_tensor(out, in0, in1, o), r, w, b)
+
+    def cp(out, in_, r, w, b=()):
+        op("V", lambda: vec.tensor_copy(out, in_), r, w, b)
+
+    def ac(out, in_, f, r, w, b=(), **kw):
+        op("A", lambda: act.activation(out, in_, f, **kw), r, w, b)
+
+    def mm(out, lhsT, rhs, start, stop, r, w, b, sig=None):
+        op("P", lambda: pe.matmul(out, lhsT, rhs, start, stop), r, w, b, sig=stop if sig is None else sig)
+
+    B = [T["B%d" % i] for i in range(8)]
+
+    dmas("mk", [("S", T.MK[:], T.mk[:])], w=["MK"])
+    dmas("su", [("S", T.SU[k:128:8, 640 * h:640 * h + 640], T.su[8 * h + k:128:16, :]) for h in range(2) for k in range(8)], w=["SU"])
+    dmas("xf", [("S", T.XT[:, 0:W], T.xf[:])], w=["XTa"])
+    dmas("pl", [("S", T.PL[:], T.pl[:])], w=["PL"])
+    dmas("sm", [("A", T.HP[:], T.hp[:]), ("A", T.CP[:], T.cp[:]), ("A", T.TH[:], T.th[:])], w=["HP", "CP", "TH"])
+    dmas("st0", [("S", T.ST[:, 0:W], T.stp[:])], w=["STa"])
+    dmas("st1", [("S", T.ST[:, H:H + W], T.stp[:]), ("S", T.ST[:, W:H], T.stp[:, 0:H - W]),
+                 ("S", T.ST[:, H + W:2 * H], T.stp[:, 0:H - W])], w=["STb"])
+
+    def iota(buf, pattern, base, cm, key):
+        if key == "PID":
+            op("G", lambda: g.iota(buf, pattern, base, cm), (), [key])
+        else:
+            op("G", lambda: g.iota(buf, pattern, base, cm, allow_small_or_imprecise_dtypes=True), (), [key])
+
+    iota(T.PID[:], [[1, 1]], 0, 1, "PID")
+    iota(T.NR[:], [[1, 160]], 0, 0, "NR")
+    iota(T.G16R[:], [[16, 8], [0, 16]], 0, 0, "G16R")
+    iota(T.PARW[:], [[0, 64], [-255, 2]], 256, 0, "PARW")
+    iota(T.JB[:], [[256, 16]], 0, 0, "JB")
+    iota(T.ZM[:], [[0, 256], [32, 8]], 0, 0, "ZM")
+
+    op("V", lambda: vec.memset(T.NEG[:], -200.0), (), ["NEG"])
+    op("V", lambda: vec.memset(T.D0[:], 0.0), (), ["D0a", "D0b", "D0c"])
+    CI, CF = T.CI, T.CF
+
+    def ci(i): return CI[:, i:i + 1]
+    def cf(i): return CF[:, i:i + 1]
+    ts(ci(0), T.PID[:], 15, None, A_.bitwise_and, None, ["PID"], ["ci0"])
+    ts(ci(1), T.PID[:], 1, None, A_.bitwise_and, None, ["PID"], ["ci1"])
+    ts(ci(2), T.PID[:], 4, 1, A_.logical_shift_right, A_.bitwise_and, ["PID"], ["ci2"])
+    ts(ci(3), T.PID[:], 112, None, A_.bitwise_and, None, ["PID"], ["ci3"])
+    ts(cf(1), T.PID[:], 16.0, None, A_.add, None, ["PID"], ["cf1"])
+    ts(cf(0), ci(1), float(H), None, A_.mult, None, ["ci1"], ["cf0"])
+    ts(cf(2), ci(3), 16.0, None, A_.add, None, ["ci3"], ["cf2"])
+    ts(cf(3), ci(3), 17.0, None, A_.add, None, ["ci3"], ["cf3"])
+    ts(cf(4), ci(0), 2.0, 1.0, A_.mult, A_.add, ["ci0"], ["cf4"])
+    ts(cf(5), ci(2), -15.0, 16.0, A_.mult, A_.add, ["ci2"], ["cf5"])
+    ts(cf(6), ci(2), 1.0, None, A_.mult, None, ["ci2"], ["cf6"])
+    ts(cf(7), ci(2), -1.0, 1.0, A_.mult, A_.add, ["ci2"], ["cf7"])
+    ts(cf(11), ci(0), 16.0, None, A_.mult, None, ["ci0"], ["cf11"])
+    ts(cf(13), ci(0), float(V), None, A_.add, None, ["ci0"], ["cf13"])
+    ts(cf(14), ci(3), 1.0, None, A_.mult, None, ["ci3"], ["cf14"])
+    tt(cf(15), cf(5), cf(2), A_.add, ["cf5", "cf2"], ["cf15"])
+
+    def band(buf, key, col, wt, lo=0, hi=160):
+        r = ["NR", "cf%d" % col] + (["cf%d" % wt] if isinstance(wt, int) else [])
+        ts(buf, T.NR[:, lo:hi], cf(col), cf(wt) if isinstance(wt, int) else wt, A_.is_equal, A_.mult, r, [key])
+
+    def scaled(out, okey, in_, key, f):
+        ac(out, in_, AF.Copy, [key], [okey], scale=f)
+
+    band(T.ID[:], "ID", 1, 1.0, 16, 144)
+    band(T.I0P[:], "I0P", 1, 7)
+    band(T.I1P[:], "I1P", 1, 6)
+    band(T.BP[:], "BP", 2, BIG)
+    ts(T.BO1[:], T.G16R[:], cf(14), 2048.0, A_.is_equal, A_.mult, ["G16R", "cf14"], ["BO1"])
+    scaled(T.IDS[:], "IDS", T.ID[:], "ID", 1.0 / 256)
+    scaled(T.ID32[:], "ID32", T.ID[:], "ID", 1.0)
+    scaled(T.I0N[:], "I0N", T.I0P[:], "I0P", -1.0)
+    scaled(T.I1N[:], "I1N", T.I1P[:], "I1P", -1.0)
+    scaled(T.BN[:], "BN", T.BP[:], "BP", -1.0)
+    scaled(T.BOP[:], "BOP", T.BO1[:], "BO1", 15.0 / 2048)
+    scaled(T.BON[:], "BON", T.BO1[:], "BO1", -15.0 / 2048)
+    band(T.WN[:], "WN", 2, 4)
+    band(T.WS[:], "WS", 15, 4)
+    band(T.LA[:], "LA", 2, 256.0)
+    band(T.LB[:], "LB", 3, 1.0)
+    band(T.ID6[:], "ID6", 1, 6.0, 16, 144)
+    tt(T.COR[:], T.BO1[:], T.PARW[:], A_.mult, ["BO1", "PARW"], ["COR"])
+    tt(T.LW[:], T.LA[:], T.LB[:], A_.add, ["LA", "LB"], ["LW"])
+    ts(T.DUM[:], T.NR[:, 0:16], 16.0, cf(13), A_.mult, A_.add, ["NR", "cf13"], ["DUM"])
+    cp(T.HF[:], T.HP[:], ["HP"], ["HF"])
+    ts(T.CAPB[:], T.CP[:], -63.5, -256.0, A_.add, A_.mult, ["CP"], ["CAPB"])
+    cp(T.THF[:], T.TH[:], ["TH"], ["THF"])
+    tt(T.D1[:], T.HF[:, 16:64], T.HF[:, 0:48], A_.subtract, ["HF"], ["D1"])
+    ts(T.KC[:, 3:64:4], T.HF[:, 0:16], 6.0, None, A_.mult, None, ["HF"], ["KC3"])
+    tt(T.D2[:], T.D1[:, 16:48], T.D1[:, 0:32], A_.subtract, ["D1"], ["D2"])
+    ts(T.KC[:, 2:64:4], T.D1[:, 0:16], 6.0, None, A_.mult, None, ["D1"], ["KC2"])
+    tt(T.KC[:, 0:64:4], T.D2[:, 16:32], T.D2[:, 0:16], A_.subtract, ["D2"], ["KC0"])
+    ts(T.KC[:, 1:64:4], T.D2[:, 0:16], 3.0, None, A_.mult, None, ["D2"], ["KC1"])
+
+    mwin = T.mm[:, 0:V]
+
+    def lanes(buf, t): return buf[:, t % Q:V:Q]
+
+    def offconv(t):
+        cp(T.OFF[:, t * L:(t + 1) * L], T.SU[:, t:V:Q], ["SU"], ["OFF%d" % t])
+
+    def succ_a(t, c):
+        c0 = (t % Q) * L + 32 * c
+        ac(T.ZA[:, 512 * c:512 * c + 512], mwin.indirect(T.OFF[:, c0:c0 + 32]), AF.Copy, ["mm", "OFF%d" % (t % Q)], ["ZA%d" % c])
+
+    def succ_v(t, c):
+        c0 = (t % Q) * L + 128 + 32 * c
+        sl = slice(512 * c, 512 * c + 512)
+        tt(T.Z[:, sl], mwin.indirect(T.OFF[:, c0:c0 + 32]), T.ZA[:, sl], A_.max, ["mm", "OFF%d" % (t % Q), "ZA%d" % c], ["Z%d" % c])
+
+    def ge8(t):
+        ac(T.GE8[:], lanes(T.mm, t), AF.Sigmoid, ["mm"], ["GE8"], bias=-1920.0, scale=256.0)
+
+    def scan():
+        op("V", lambda: vec.tensor_tensor_scan(T.Z2[:], T.ZM[:], T.Z[:], 0.0, A_.min, A_.max), ["ZM", "Z0", "Z1", "Z2", "Z3"], ["ZS"])
+
+    def g4():
+        for l2 in range(2):
+            ac(B[7][:, L + 128 * l2:L + 128 * l2 + 128], T.Z2[:, 7 + 8 * l2:2048:16], AF.Identity, ["ZS"], ["BM"], ["B7"], bias=-4.0)
+
+    def gx(q, t, lo, hi):
+        end = H + W if t == 0 else 2 * H
+        r = ["XTa", "XTb", "XTc", "LST"] + ([] if t == 0 else ["XTd"])
+        src = T.XT[:, 0:end].indirect(T.LST[:, lo:hi])
+        out = T.XK[:, 16 * lo:16 * hi]
+        keys = ["XK%d" % i for i in range(lo // 32, hi // 32)]
+        if q == "V": cp(out, src, r, keys)
+        else: ac(out, src, AF.Copy, r, keys)
+
+    def xk(c, a): return T.XK[:, 1024 * c + a:1024 * c + 1024:16]
+
+    def pe_sum(c):
+        for a in range(16):
+            mm(B[4][:, 64 * c:64 * c + 64], (T.IDS if a & 1 else T.ID)[:], xk(c, a), a == 0, a == 15,
+               ["XK%d" % (2 * c), "XK%d" % (2 * c + 1), "ID", "IDS"], ["S%d" % c], ["B4"])
+
+    def pe_pack(cs, qs):
+        for q in qs:
+            for c in cs:
+                o = B[q // 2][:, (q % 2) * L + 64 * c:(q % 2) * L + 64 * c + 64]
+                for e in range(2):
+                    mm(o, T.ID[:], xk(c, 2 * q + e), e == 0, e == 1, ["XK%d" % (2 * c), "XK%d" % (2 * c + 1), "ID"],
+                       ["PK%d_%d" % (q, c)], ["B%d" % (q // 2)], sig=(e == 1 and q % 2 == 1 and c == cs[-1]))
+
+    def gs(t, c):
+        if t == 0:
+            src, r = T.ST[:, 0:W].indirect(T.LS0[:, 64 * c:64 * c + 64]), ["STa", "LS0"]
+        else:
+            src, r = T.ST[:].indirect(T.LST[:, 64 * c:64 * c + 64]), ["STa", "STb", "LST"]
+        ac(T.SK[:, 1024 * c:1024 * c + 1024], src, AF.Copy, r, ["SK%d" % c])
+
+    def tr(c):
+        sl = slice(1024 * c, 1024 * c + 1024)
+        op("V", lambda: vec.transpose(T.TR[:, sl], T.SK[:, sl]), ["SK%d" % c], ["TR%d" % c])
+
+    SKEYS = ["S%d" % c for c in range(4)]
+    TRK = ["TR%d" % c for c in range(4)]
+
+    def prod(q):
+        tt(T.PR[:, q * L:(q + 1) * L], B[q // 2][:, (q % 2) * L:(q % 2 + 1) * L], T.OV[:], A_.mult,
+           ["PK%d_%d" % (q, c) for c in range(4)] + ["OV"], ["PR%d" % q], ["B%d" % (q // 2)])
+        if q == 0:
+            mm(B[4][:, L:2 * L], T.COR[:], T.OV[:], True, False, ["COR", "OV"], ["TT"], ["B4"])
+        mm(B[4][:, L:2 * L], T.LW[:, 16 - 2 * q:144 - 2 * q], T.PR[:, q * L:(q + 1) * L], False, q == 7,
+           ["LW", "PR%d" % q], ["TT"], ["B4"])
+
+    def turn(out, mats, keys, rhs, rkeys, start, stop, wkey, bk, sig=None):
+        for h in range(2):
+            for gp in range(2):
+                o = 16 - 16 * (gp - h)
+                mm(out(h), mats[h][:, o:o + 128], rhs(gp), start and gp == 0, stop and gp == 1, rkeys + keys, [wkey(h)], [bk(h)],
+                   sig=None if sig is None else (h == 1 and gp == 1))
+
+    ac(mwin, T.MK[:], AF.Copy, ["MK"], ["mm"])
+    ge8(0)
+    offconv(0)
+    for c in range(4):
+        succ_a(0, c)
+        succ_v(0, c)
+    ts(T.XT[:, H:H + W], T.XT[:, 0:W], -8.0, 256.0, A_.add, A_.mult, ["XTa"], ["XTc"])
+    ac(T.XT[:, W:H], T.XT[:, 0:H - W], AF.Copy, ["XTa"], ["XTb"])
+    scan()
+    g4()
+    ts(T.LST[:], T.PL[:, 0:V:Q], cf(0), None, A_.add, None, ["PL", "cf0"], ["LST"])
+
+    for t in range(RO):
+        d = cores[(rank + 1 + t % (n - 1)) % n]
+        s_ = cores[(rank - 1 - t % (n - 1)) % n]
+        first, final = t == 0, t == RO - 1
+        ml = lanes(T.mm, t)
+        for c in range(3):
+            gx("A", t, 64 * c, 64 * c + 32)
+            gx("V", t, 64 * c + 32, 64 * c + 64)
+            pe_sum(c)
+            pe_pack([c], range(8 if c < 2 else 4))
+        if first:
+            gx("A", t, 192, 224)
+            gx("V", t, 224, 256)
+            cp(T.LS0[:], T.PL[:, 0:V:Q], ["PL"], ["LS0"])
+            cp(T.pp[:, 0:V], T.PL[:], ["PL"], ["pp"])
+        else:
+            gx("A", t, 192, 256)
+            for c in range(N1, 4): succ_v(t, c)
+            scan()
+        pe_sum(3)
+        pe_pack([3], range(4))
+        pe_pack([2, 3], range(4, 8))
+        ac(T.OV[:], B[4][:, 0:L], AF.Sigmoid, SKEYS + ["BIAS", "CAPB"], ["OV"], ["B4"],
+           bias=(T.CAPB if first else T.BIAS)[:], scale=256.0)
+        ac(T.SB[:], B[4][:, 0:L], AF.Identity, SKEYS, ["SB"], ["B4"], bias=64.0)
+        if not first: g4()
+        for c in range(4): gs(t, c)
+        for p in range(16):
+            mm(B[5][:, 0:16], T.WN[:, 16 - p:144 - p], T.SB[:, p:L:16], p == 0, p == 15, ["WN", "SB"], ["UP"], ["B5"])
+        for q in range(4): prod(q)
+        cp(T.U[:, 0:16], B[5][:, 0:16], ["UP"], ["U"], ["B5"])
+        for r_ in range(16):
+            sh = 16 * (r_ & 1) + 2 * (r_ >> 1)
+            mm(B[5][:, 16:32], T.WS[:, 32 - sh:160 - sh], T.SB[:, r_:L:16], r_ == 0, r_ == 15, ["WS", "SB"], ["UQ"], ["B5"])
+        prod(4)
+        ts(T.BB[:], T.U[:, 0:16], 4, 3, A_.logical_shift_right, A_.bitwise_and, ["U"], ["BB"])
+        prod(5)
+        for i, key in ((1, "D0a"), (2, "D0b"), (3, "D0c")):
+            ts(T.D0[:, i:64:4], T.BB[:], float(i - 3), None, A_.add, None, ["BB"], [key])
+        op("V", lambda: vec.tensor_tensor_scan(T.C6[:], T.D0[:], T.KC[:], 0.0, A_.mult, A_.add),
+           ["D0a", "D0b", "D0c", "KC0", "KC1", "KC2", "KC3"], ["C6"])
+        prod(6)
+        ts(T.cS[:, 16 * t:16 * t + 16], T.C6[:, 3:64:4], 1.0 / 6, 0.25, A_.mult, A_.add, ["C6"], ["cS%d" % t])
+        send("c", t, d, 16)
+        prod(7)
+        cp(T.U[:, 16:32], B[5][:, 16:32], ["UQ"], ["U2"], ["B5"])
+        tt(T.NEWA[:], B[7][:, L:2 * L], ml, A_.max, ["BM", "mm"], ["NEWA"], ["B7"])
+        mm(B[5][:, 32:48], T.ID6[:], T.DUM[:], True, False, ["ID6", "DUM"], ["OL"], ["B5"])
+        for p in range(16):
+            mm(B[5][:, 32:48], T.BP[:, 16 - p:144 - p], T.GE8[:, p:L:16], False, False, ["BP", "GE8"], ["OL"], ["B5"])
+        mm(B[6][:, 0:L], T.BON[:], T.GE8[:], True, False, ["BON", "GE8"], ["CN"], ["B6"], sig=True)
+        mm(B[1][:, 0:L], T.ID32[:], lanes(T.pp, t), True, False, ["ID32", "pp"], ["X"], ["B1"], sig=True)
+        cp(T.TI[:], B[4][:, L:2 * L], ["TT"], ["TI"], ["B4"])
+        ts(T.J1[:], T.U[:, 16:32], 15, None, A_.bitwise_and, None, ["U2"], ["J1"])
+        ts(T.LI[:], T.TI[:], 8, 255, A_.logical_shift_right, A_.bitwise_and, ["TI"], ["LI"])
+        ts(T.J2[:], T.J1[:], 1.0, cf(11), A_.max, A_.add, ["J1", "cf11"], ["J2"])
+        ts(B[7][:, 0:L], T.LI[:], T.THF[:, t:t + 1], 15.0, A_.is_ge, A_.mult, ["LI", "THF"], ["F15"], ["B7"])
+        tt(T.J3[:], T.J2[:], T.JB[:], A_.add, ["J2", "JB"], ["J3"])
+        tt(ml, B[7][:, 0:L], T.NEWA[:], A_.max, ["F15", "NEWA"], ["mm"], ["B7"])
+        cp(T.JL[:], T.J3[:], ["J3"], ["JL"])
+        ts(T.HI[:], ml, 8.0, None, A_.is_ge, None, ["mm"], ["HI"])
+        for p in range(16):
+            mm(B[5][:, 32:48], T.BN[:, 16 - p:144 - p], T.HI[:, p:L:16], False, p == 15, ["BN", "HI"], ["OL"], ["B5"])
+        mm(B[6][:, 0:L], T.BOP[:], T.HI[:], False, True, ["BOP", "HI"], ["CN"], ["B6"])
+
+        def back():
+            ts(T.bS[:, t * L:(t + 1) * L], mwin.indirect(T.cR[:, 16 * t:16 * t + 16]), -4.0, None, A_.add, None,
+               ["mm", "cR%d" % t], ["bS%d" % t])
+            send("b", t, s_, L)
+
+        if final: tr(0)
+        else: back()
+        tt(T.L6[:], B[5][:, 32:48], T.C6[:, 3:64:4], A_.max, ["OL", "C6"], ["L6"], ["B5"])
+        ts(T.lS[:, 16 * t:16 * t + 16], T.L6[:], 1.0 / 6, 0.25, A_.mult, A_.add, ["L6"], ["lS%d" % t])
+        send("l", t, d, 16)
+        if not final: tr(0)
+        if not final:
+            ac(T.JK[:], B[6][:, 0:L], AF.Sigmoid, ["CN"], ["JK", "AC"], ["B6"], bias=-128.0, scale=256.0, accum_out=T.AC[:])
+        tr(1)
+        tr(2)
+        ac(T.SJ[:, 0:192], T.TR[:, 0:3072].indirect(T.JL[:, 0:12]), AF.Copy, TRK[:3] + ["JL"], ["SJ"])
+        tr(3)
+        ac(T.SJ[:, 192:L], T.TR[:].indirect(T.JL[:, 12:16]), AF.Copy, TRK + ["JL"], ["SJ"])
+        turn(lambda h: B[2 * h][:, 0:128], (T.I0N, T.I1N), ["I0N", "I1N"], lambda gp: T.TR[:, 16 * gp:4096:32], TRK,
+             True, False, lambda h: "DD%d" % h, lambda h: "B%d" % (2 * h))
+        turn(lambda h: B[2 * h][:, 0:128], (T.I0P, T.I1P), ["I0P", "I1P"], lambda gp: T.SJ[:, gp:L:2], ["SJ"],
+             False, True, lambda h: "DD%d" % h, lambda h: "B%d" % (2 * h))
+        turn(lambda h: B[1][:, h:L:2], (T.I0P, T.I1P), ["I0P", "I1P"], lambda gp: T.TR[:, 16 * gp:4096:32], TRK,
+             False, False, lambda h: "X", lambda h: "B1", sig=True)
+        if not final:
+            cp(T.AI[:], T.AC[:], ["AC"], ["AI"])
+            if first:
+                ts(T.XT[:, H + W:2 * H], T.XT[:, H:2 * H - W], 1.0, None, A_.mult, None, ["XTc"], ["XTd"])
+            if t + 1 < Q: offconv(t + 1)
+            ts(T.A7[:], T.AI[:], 7, None, A_.bitwise_and, None, ["AI"], ["A7"])
+            ts(T.BIAS[:], T.A7[:], -256.0, T.CAPB[:], A_.mult, A_.add, ["A7", "CAPB"], ["BIAS"])
+        else:
+            back()
+            ac(T.FL[:], T.pp[:, 0:V], AF.Sigmoid, ["pp"], ["FL"], bias=-256.0 * (W - 0.5), scale=256.0)
+        for h in range(2):
+            tt(T.HD[:, h:L:2], B[2 * h][:, 0:128], T.HI[:, h:L:2], A_.mult, ["DD%d" % h, "HI"], ["HD%d" % h], ["B%d" % (2 * h)])
+        mm(B[1][:, 0:L], T.ID[:], T.HD[:], False, True, ["ID", "HD0", "HD1"], ["X"], ["B1"])
+        ks = T.kS[:, t * L:(t + 1) * L]
+        if not final:
+            cp(ks, B[1][:, 0:L], ["X"], ["kS%d" % t], ["B1"])
+        else:
+            ts(T.WF[:], B[1][:, 0:L], float(W), float(W), A_.is_ge, A_.mult, ["X"], ["WF"], ["B1"])
+            tt(T.WY[:], B[1][:, 0:L], T.WF[:], A_.subtract, ["X", "WF"], ["WY"], ["B1"])
+            cp(ks, T.WY[:], ["WY"], ["kS%d" % t])
+        send("k", t, d, L)
+        ac(T.mm[:].indirect(T.lR[:, 16 * t:16 * t + 16]), T.NEG[:], AF.Sigmoid, ["NEG", "lR%d" % t], ["mm"])
+        if final:
+            pieces = [(3, 0, 512), (4, 512, 1024), (5, 1024, V)]
+            for bk, lo, hi_ in pieces:
+                ac(B[bk][:, 0:hi_ - lo], T.FL[:, lo:hi_], AF.Copy, ["FL"], ["NF%d" % bk], ["B%d" % bk], scale=-float(W))
+        tt(B[7][:, L:2 * L], B[6][:, 0:L], T.bR[:, t * L:(t + 1) * L], A_.min, ["CN", "bR%d" % t], ["BM"], ["B6", "B7"])
+        tt(ml, B[7][:, L:2 * L], ml, A_.max, ["BM", "mm"], ["mm"], ["B7"])
+        if not final:
+            for c in range(4): succ_a(t + 1, c)
+            ge8(t + 1)
+            for c in range(N1): succ_v(t + 1, c)
+        else:
+            ac(T.MK[:], mwin, AF.Copy, ["mm"], ["MK"])
+            dmas("ymk", [("S", T.ymk[:], T.MK[:])], r=["MK"])
+            for bk, lo, hi_ in pieces:
+                tt(T.pp[:, lo:hi_], B[bk][:, 0:hi_ - lo], T.pp[:, lo:hi_], A_.add, ["NF%d" % bk, "pp"], ["pp%d" % bk], ["B%d" % bk])
+        cp(T.pp[:].indirect(T.lR[:, 16 * t:16 * t + 16]), T.kR[:, t * L:(t + 1) * L], ["lR%d" % t, "kR%d" % t],
+           ["pp"] + (["pp3", "pp4", "pp5"] if final else []))
+        if not final:
+            ts(T.LST[:], lanes(T.pp, t + 1), cf(0), None, A_.add, None, ["pp", "cf0"], ["LST"])
+    dmas("ypl", [("S", T.ypl[:], T.pp[:, 0:V])], r=["pp"])
+    for s, v in total.items():
+        if known["G"].get(s, 0) < v:
+            g.wait_ge(T.sem[s], v)

@@ -3,38 +3,54 @@ from concourse.mybir import dt, AluOpType, AxisListType, ActivationFunctionType
 
 W, V, Q, L, RO = 2816, 1280, 5, 256, 6
 H = 4096
-N1 = 2
+PK = 241
 BIG = 16384.0
+PAIRS = 8
+
+LOADS = "sm pl0 xf pl1 mk su0 su1 st xw"
+FIRST = """list0 x0:A x1:V targets list1 sum0 x2:A x3:V sum1 x4:A x5:V x6:A x7:V levels:A sum2 sum3 pack0 ov ge8:A sb own off0
+za0:A za1:A za2:A za3:V off1 s0:A s1:A s2:A s3:A s4:A pack1 pr0 pr1 pr2 pr3 pu u pack2 bb d0 c6 cs sendc pr4 pr5 pr6 pr7 j1 j2
+zv0 zv1 zv2 zv3 t0 t1 t2 t3 t4 open olg pj t5 t6 t7 jl scan g4 rq:A r2 s5:A s6:A s7:A tr0 newa f na8:V hf ol tr1 ml back:A pick0 cn
+turn0 l6 ls sendl sendb tr2 tr3 hd0 jk pick1 off ai xs0 ks0 turn1 hd1 xs1 a7 ks1 sendk places zero bm step4"""
+FRONT = """za0:V za1:A ge8:A za2:A za3:A olg zv0 land list x0:A x1:V sum0 x2:A x3:V sum1 pack0 x4:A x5:V sum2 x6:A x7:A sum3
+zv1 zv2 zv3 s0:A ov sb scan pack1 pr0 pr1 pr2 pr3 s1:A s2:A s3:A s4:A pu u bb j1 pack2 t0 t1 g4 d0 j2 pr4 c6 pr5 cs sendc pr6
+t2 t3 t4 t5 t6 pr7 t7 pj tr0 newa na8:V rq:A r2 f """
+MIDDLE = FRONT + """hf tr1 ml ol cn open l6 jl ls sendl back:V sendb s5:A s6:A s7:A pick0 jk turn0 tr2 tr3 hd0 ai off a7
+pick1 turn1 hd1 xs0 ks0 xs1 ks1 sendk zero bm step4"""
+LAST = FRONT + """open jl hf ol tr1 ml cn l6 s5:A s6:A pick0 s7:A ls back:A turn0 tr2 hd0 sendl tr3 sendb pick1 jk zero xs0 turn1
+ks0 hd1 sendk0 xs1 ks1 sendk1 bm wrap0 step4 wrap1 wrap2 outm land0 land1 outp"""
 
 F32, BF, F16, I32, U16 = "float32", "bfloat16", "float16", "int32", "uint16"
 SCRATCH = {
-    "XT": ("sbuf", [128, 2 * H], BF), "ST": ("sbuf", [128, 2 * H], BF),
+    "XT": ("sbuf", [128, H], BF), "ST": ("sbuf", [128, H], BF),
     "XK": ("sbuf", [128, 4096], BF), "SK": ("sbuf", [128, 4096], BF), "TR": ("sbuf", [128, 4096], BF),
     "PR": ("sbuf", [128, 2048], F16),
     "pp": ("sbuf", [128, V + L], F32), "mm": ("sbuf", [128, V + L], F32),
     "PL": ("sbuf", [128, V], I32), "SU": ("sbuf", [128, V], I32), "MK": ("sbuf", [128, V], BF),
-    "OFF": ("sbuf", [128, V], U16), "LST": ("sbuf", [128, L], U16), "LS0": ("sbuf", [128, L], U16),
+    "OFF": ("sbuf", [128, V], U16), "LST": ("sbuf", [128, L], U16),
     "ZA": ("sbuf", [128, 2048], BF), "Z": ("sbuf", [128, 2048], BF), "Z2": ("sbuf", [128, 2048], BF), "ZM": ("sbuf", [128, 2048], BF),
     "GE8": ("sbuf", [128, L], BF), "NEWA": ("sbuf", [128, L], BF), "HI": ("sbuf", [128, L], BF),
     "OV": ("sbuf", [128, L], BF), "SB": ("sbuf", [128, L], BF), "SJ": ("sbuf", [128, L], BF), "HD": ("sbuf", [128, L], BF),
-    "JK": ("sbuf", [128, L], BF), "NEG": ("sbuf", [128, L], F32),
-    "TI": ("sbuf", [128, L], I32), "LI": ("sbuf", [128, L], I32),
-    "WF": ("sbuf", [128, L], F32), "WY": ("sbuf", [128, L], F32), "FL": ("sbuf", [128, V], BF),
+    "JK": ("sbuf", [128, L], BF), "NEG": ("sbuf", [128, L], F32), "RQ": ("sbuf", [128, L], F16), "R2": ("sbuf", [128, L], F32),
+    "ONE": ("sbuf", [128, L], BF), "WF": ("sbuf", [128, L], F32), "WY": ("sbuf", [128, L], F32),
     "HP": ("sbuf", [128, 64], I32), "HF": ("sbuf", [128, 64], F32), "D1": ("sbuf", [128, 48], F32), "D2": ("sbuf", [128, 32], F32),
     "KC": ("sbuf", [128, 64], F32), "D0": ("sbuf", [128, 64], F32), "C6": ("sbuf", [128, 64], F32),
     "CP": ("sbuf", [128, 1], I32), "TH": ("sbuf", [128, RO], I32), "THF": ("sbuf", [128, RO], F32),
     "CAPB": ("sbuf", [128, 1], F32), "BIAS": ("sbuf", [128, 1], F32), "AC": ("sbuf", [128, 1], F32),
     "AI": ("sbuf", [128, 1], I32), "A7": ("sbuf", [128, 1], I32),
-    "U": ("sbuf", [128, 32], I32), "BB": ("sbuf", [128, 16], I32), "J1": ("sbuf", [128, 16], I32),
-    "J2": ("sbuf", [128, 16], F32), "J3": ("sbuf", [128, 16], F32), "JL": ("sbuf", [128, 16], U16), "L6": ("sbuf", [128, 16], F32),
+    "U": ("sbuf", [128, 16], I32), "BB": ("sbuf", [128, 16], I32), "J1": ("sbuf", [128, 16], I32),
+    "J2": ("sbuf", [128, 16], F16), "JL": ("sbuf", [128, 16], U16), "L6": ("sbuf", [128, 16], F32),
     "PID": ("sbuf", [128, 1], I32), "CI": ("sbuf", [128, 8], I32), "CF": ("sbuf", [128, 16], F32),
-    "NR": ("sbuf", [128, 160], F32), "G16R": ("sbuf", [128, 128], F32), "PARW": ("sbuf", [128, 128], F32),
-    "WN": ("sbuf", [128, 160], BF), "WS": ("sbuf", [128, 160], BF), "BP": ("sbuf", [128, 160], BF), "BN": ("sbuf", [128, 160], BF),
+    "NR": ("sbuf", [128, 160], F32), "G16R": ("sbuf", [128, 128], F32),
+    "WN": ("sbuf", [128, 160], BF), "BP": ("sbuf", [128, 160], BF), "BN": ("sbuf", [128, 160], BF),
     "LW": ("sbuf", [128, 160], F16), "LA": ("sbuf", [128, 160], F32), "LB": ("sbuf", [128, 160], F32),
     "I0P": ("sbuf", [128, 160], BF), "I1P": ("sbuf", [128, 160], BF), "I0N": ("sbuf", [128, 160], BF), "I1N": ("sbuf", [128, 160], BF),
-    "ID": ("sbuf", [128, 128], BF), "IDS": ("sbuf", [128, 128], BF), "ID32": ("sbuf", [128, 128], F32), "ID6": ("sbuf", [128, 128], F16),
+    "ID": ("sbuf", [128, 128], BF), "IDK": ("sbuf", [128, 128], BF), "ID32": ("sbuf", [128, 128], F32), "ID6": ("sbuf", [128, 128], F16),
+    "IDM4": ("sbuf", [128, 128], BF), "ID0": ("sbuf", [128, 128], BF), "ID16": ("sbuf", [128, 128], BF), "AR": ("sbuf", [128, 128], F32),
+    "LW1": ("sbuf", [128, 160], BF), "LWK": ("sbuf", [128, 160], BF), "RL": ("sbuf", [128, 1024], BF), "NA8": ("sbuf", [128, L], BF),
+    "IDH": ("sbuf", [128, 128], F16), "PERM": ("sbuf", [128, 128], F16),
     "BOP": ("sbuf", [128, 128], BF), "BON": ("sbuf", [128, 128], BF), "BO1": ("sbuf", [128, 128], F32), "COR": ("sbuf", [128, 128], BF),
-    "JB": ("sbuf", [128, 16], F32), "DUM": ("sbuf", [128, 16], F16),
+    "JB": ("sbuf", [128, 16], F16), "DUM": ("sbuf", [128, 16], F16),
     "cS": ("sbuf", [128, RO * 16], U16), "cR": ("sbuf", [128, RO * 16], U16),
     "lS": ("sbuf", [128, RO * 16], U16), "lR": ("sbuf", [128, RO * 16], U16),
     "bS": ("sbuf", [128, RO * L], BF), "bR": ("sbuf", [128, RO * L], BF),
@@ -43,9 +59,9 @@ SCRATCH = {
 for _b in range(8):
     SCRATCH["B%d" % _b] = ("psum", [128, 512], F32)
 
-DMAS = ["pl", "xf", "mk", "su", "st0", "st1", "sm", "ypl", "ymk"]
+DMAS = ["pl0", "pl1", "xf", "mk", "su0", "su1", "sm", "st", "xw", "ypl", "ymk"]
 SEMAPHORES = ["cV", "cA", "cP", "cG", "sent"] + ["d_" + n for n in DMAS] + \
-             ["r%s%d" % (k, t) for k in "clbk" for t in range(RO)]
+             ["r%s%d" % (k, t) for k in "clbkj" for t in range(RO)]
 
 
 def rank_program(g, core, T, topo):
@@ -120,20 +136,14 @@ def rank_program(g, core, T, topo):
 
     neng = min(len(topo.engines(a, b)) for a in cores for b in cores if a != b)
 
-    def send(kind, t, dst, width):
-        key = "%sS%d" % (kind, t)
-        wait("G", deps("G", [key], (), ()))
+    def send(kind, sem, dst, lo, hi, r):
+        wait("G", deps("G", r, (), ()))
         rid, pid, _ = topo.addr(dst)
         mask = sum(1 << e for e in topo.engines(core, dst)[:neng])
-        sl = slice(t * width, (t + 1) * width)
-        g.remote_dma(T[kind + "R"][:, sl], T[kind + "S"][:, sl], T.sem["r%s%d" % (kind, t)], T.sem.sent, pid, rid, mask)
+        g.remote_dma(T[kind + "R"][:, lo:hi], T[kind + "S"][:, lo:hi], T.sem[sem], T.sem.sent, pid, rid, mask)
         total["sent"] = total.get("sent", 0) + neng
-
-    for kind in "clbk":
-        for t in range(RO):
-            s = "r%s%d" % (kind, t)
-            lastw["%sR%d" % (kind, t)] = (s, neng, {})
-            total[s] = neng
+        lastw[sem] = (sem, neng, {})
+        total[sem] = neng
 
     vec, act, pe = g.vector, g.scalar, g.tensor
 
@@ -156,15 +166,25 @@ def rank_program(g, core, T, topo):
         op("P", lambda: pe.matmul(out, lhsT, rhs, start, stop), r, w, b, sig=stop if sig is None else sig)
 
     B = [T["B%d" % i] for i in range(8)]
+    pS = pG = pBM = B[4][:, 0:L]
+    pU, pJ, pOL = B[4][:, L:L + 16], B[4][:, L + 16:L + 32], B[5][:, 0:16]
+    pT, pCN, pF = B[6][:, 0:L], B[6][:, L:2 * L], B[7][:, 0:L]
 
-    dmas("mk", [("S", T.MK[:], T.mk[:])], w=["MK"])
-    dmas("su", [("S", T.SU[k:128:8, 640 * h:640 * h + 640], T.su[8 * h + k:128:16, :]) for h in range(2) for k in range(8)], w=["SU"])
-    dmas("xf", [("S", T.XT[:, 0:W], T.xf[:])], w=["XTa"])
-    dmas("pl", [("S", T.PL[:], T.pl[:])], w=["PL"])
-    dmas("sm", [("A", T.HP[:], T.hp[:]), ("A", T.CP[:], T.cp[:]), ("A", T.TH[:], T.th[:])], w=["HP", "CP", "TH"])
-    dmas("st0", [("S", T.ST[:, 0:W], T.stp[:])], w=["STa"])
-    dmas("st1", [("S", T.ST[:, H:H + W], T.stp[:]), ("S", T.ST[:, W:H], T.stp[:, 0:H - W]),
-                 ("S", T.ST[:, H + W:2 * H], T.stp[:, 0:H - W])], w=["STb"])
+    def load(name):
+        if name == "mk": dmas("mk", [("S", T.MK[:], T.mk[:])], w=["MK"])
+        if name == "xf": dmas("xf", [("S", T.XT[:, 0:W], T.xf[:])], w=["XTa"])
+        if name == "st": dmas("st", [("S", T.ST[:, 0:W], T.stp[:])], w=["STa"])
+        if name == "sm": dmas("sm", [("A", T.HP[:], T.hp[:]), ("A", T.CP[:], T.cp[:]), ("A", T.TH[:], T.th[:])], w=["HP", "CP", "TH"])
+        if name == "xw": dmas("xw", [("S", T.XT[:, W:H], T.xf[:, 0:H - W]), ("S", T.ST[:, W:H], T.stp[:, 0:H - W])], w=["XTb", "STb"])
+        if name[:2] == "pl":
+            lo, hi = (0, 320) if name == "pl0" else (320, V)
+            dmas(name, [("S", T.PL[:, lo:hi], T.pl[:, lo:hi])], w=["PL" + name[2]])
+        if name[:2] == "su":
+            h = int(name[2])
+            dmas(name, [("S", T.SU[k:128:8, 640 * h:640 * h + 640], T.su[8 * h + k:128:16, :]) for k in range(8)], w=["SU%d" % h])
+
+    for name in LOADS.split():
+        load(name)
 
     def iota(buf, pattern, base, cm, key):
         if key == "PID":
@@ -175,12 +195,12 @@ def rank_program(g, core, T, topo):
     iota(T.PID[:], [[1, 1]], 0, 1, "PID")
     iota(T.NR[:], [[1, 160]], 0, 0, "NR")
     iota(T.G16R[:], [[16, 8], [0, 16]], 0, 0, "G16R")
-    iota(T.PARW[:], [[0, 64], [-255, 2]], 256, 0, "PARW")
-    iota(T.JB[:], [[256, 16]], 0, 0, "JB")
+    iota(T.AR[:], [[0, 8], [1, 16]], 0, 0, "AR")
     iota(T.ZM[:], [[0, 256], [32, 8]], 0, 0, "ZM")
 
     op("V", lambda: vec.memset(T.NEG[:], -200.0), (), ["NEG"])
-    op("V", lambda: vec.memset(T.D0[:], 0.0), (), ["D0a", "D0b", "D0c"])
+    op("V", lambda: vec.memset(T.ONE[:], 1.0), (), ["ONE"])
+    op("V", lambda: vec.memset(T.D0[:], 0.0), (), ["D0"])
     CI, CF = T.CI, T.CF
 
     def ci(i): return CI[:, i:i + 1]
@@ -190,17 +210,19 @@ def rank_program(g, core, T, topo):
     ts(ci(2), T.PID[:], 4, 1, A_.logical_shift_right, A_.bitwise_and, ["PID"], ["ci2"])
     ts(ci(3), T.PID[:], 112, None, A_.bitwise_and, None, ["PID"], ["ci3"])
     ts(cf(1), T.PID[:], 16.0, None, A_.add, None, ["PID"], ["cf1"])
-    ts(cf(0), ci(1), float(H), None, A_.mult, None, ["ci1"], ["cf0"])
+    ts(cf(0), ci(1), -float(PK), float(PK), A_.mult, A_.add, ["ci1"], ["cf0"])
     ts(cf(2), ci(3), 16.0, None, A_.add, None, ["ci3"], ["cf2"])
     ts(cf(3), ci(3), 17.0, None, A_.add, None, ["ci3"], ["cf3"])
     ts(cf(4), ci(0), 2.0, 1.0, A_.mult, A_.add, ["ci0"], ["cf4"])
-    ts(cf(5), ci(2), -15.0, 16.0, A_.mult, A_.add, ["ci2"], ["cf5"])
+    tt(cf(5), ci(1), ci(2), A_.subtract, ["ci1", "ci2"], ["cf5"])
     ts(cf(6), ci(2), 1.0, None, A_.mult, None, ["ci2"], ["cf6"])
     ts(cf(7), ci(2), -1.0, 1.0, A_.mult, A_.add, ["ci2"], ["cf7"])
+    ts(cf(8), ci(1), PK - 1.0, 1.0, A_.mult, A_.add, ["ci1"], ["cf8"])
+    ts(cf(9), cf(0), -1280.0, None, A_.mult, None, ["cf0"], ["cf9"])
     ts(cf(11), ci(0), 16.0, None, A_.mult, None, ["ci0"], ["cf11"])
     ts(cf(13), ci(0), float(V), None, A_.add, None, ["ci0"], ["cf13"])
     ts(cf(14), ci(3), 1.0, None, A_.mult, None, ["ci3"], ["cf14"])
-    tt(cf(15), cf(5), cf(2), A_.add, ["cf5", "cf2"], ["cf15"])
+    ts(cf(15), cf(5), 15.0, cf(1), A_.mult, A_.add, ["cf5", "cf1"], ["cf15"])
 
     def band(buf, key, col, wt, lo=0, hi=160):
         r = ["NR", "cf%d" % col] + (["cf%d" % wt] if isinstance(wt, int) else [])
@@ -213,254 +235,238 @@ def rank_program(g, core, T, topo):
     band(T.I0P[:], "I0P", 1, 7)
     band(T.I1P[:], "I1P", 1, 6)
     band(T.BP[:], "BP", 2, BIG)
-    ts(T.BO1[:], T.G16R[:], cf(14), 2048.0, A_.is_equal, A_.mult, ["G16R", "cf14"], ["BO1"])
-    scaled(T.IDS[:], "IDS", T.ID[:], "ID", 1.0 / 256)
-    scaled(T.ID32[:], "ID32", T.ID[:], "ID", 1.0)
+    ts(T.BO1[:], T.G16R[:], cf(14), 1.0, A_.is_equal, A_.mult, ["G16R", "cf14"], ["BO1"])
+    for out, key, f in ((T.IDK, "IDK", PK), (T.ID32, "ID32", 1), (T.IDM4, "IDM4", -0.25), (T.ID0, "ID0", 0), (T.ID16, "ID16", 16)):
+        scaled(out[:], key, T.ID[:], "ID", float(f))
     scaled(T.I0N[:], "I0N", T.I0P[:], "I0P", -1.0)
     scaled(T.I1N[:], "I1N", T.I1P[:], "I1P", -1.0)
     scaled(T.BN[:], "BN", T.BP[:], "BP", -1.0)
-    scaled(T.BOP[:], "BOP", T.BO1[:], "BO1", 15.0 / 2048)
-    scaled(T.BON[:], "BON", T.BO1[:], "BO1", -15.0 / 2048)
+    ac(T.BOP[:], T.BO1[:], AF.Sigmoid, ["BO1"], ["BOP"], bias=-128.0, scale=256.0)
+    scaled(T.BON[:], "BON", T.BO1[:], "BO1", -1.0)
+    ts(T.AR[:], T.AR[:], 2.0 * PAIRS, 8.0 * (PK + 1), A_.is_lt, A_.mult, ["AR"], ["AR"])
+    tt(T.COR[:], T.BO1[:], T.AR[:], A_.mult, ["BO1", "AR"], ["COR"])
     band(T.WN[:], "WN", 2, 4)
-    band(T.WS[:], "WS", 15, 4)
-    band(T.LA[:], "LA", 2, 256.0)
+    band(T.LA[:], "LA", 2, 1.0)
     band(T.LB[:], "LB", 3, 1.0)
     band(T.ID6[:], "ID6", 1, 6.0, 16, 144)
-    tt(T.COR[:], T.BO1[:], T.PARW[:], A_.mult, ["BO1", "PARW"], ["COR"])
+    band(T.IDH[:], "IDH", 1, 1.0, 16, 144)
+    band(T.PERM[:], "PERM", 15, 1.0, 16, 144)
     tt(T.LW[:], T.LA[:], T.LB[:], A_.add, ["LA", "LB"], ["LW"])
+    if PAIRS < 8:
+        for out, key, f in ((T.LW1, "LW1", 1.0), (T.LWK, "LWK", float(PK))):
+            ts(out[:], T.LW[:], f, None, A_.mult, None, ["LW"], [key])
     ts(T.DUM[:], T.NR[:, 0:16], 16.0, cf(13), A_.mult, A_.add, ["NR", "cf13"], ["DUM"])
-    cp(T.HF[:], T.HP[:], ["HP"], ["HF"])
-    ts(T.CAPB[:], T.CP[:], -63.5, -256.0, A_.add, A_.mult, ["CP"], ["CAPB"])
-    cp(T.THF[:], T.TH[:], ["TH"], ["THF"])
-    tt(T.D1[:], T.HF[:, 16:64], T.HF[:, 0:48], A_.subtract, ["HF"], ["D1"])
-    ts(T.KC[:, 3:64:4], T.HF[:, 0:16], 6.0, None, A_.mult, None, ["HF"], ["KC3"])
-    tt(T.D2[:], T.D1[:, 16:48], T.D1[:, 0:32], A_.subtract, ["D1"], ["D2"])
-    ts(T.KC[:, 2:64:4], T.D1[:, 0:16], 6.0, None, A_.mult, None, ["D1"], ["KC2"])
-    tt(T.KC[:, 0:64:4], T.D2[:, 16:32], T.D2[:, 0:16], A_.subtract, ["D2"], ["KC0"])
-    ts(T.KC[:, 1:64:4], T.D2[:, 0:16], 3.0, None, A_.mult, None, ["D2"], ["KC1"])
+    ts(T.JB[:], T.NR[:, 0:16], 256.0, cf(11), A_.mult, A_.add, ["NR", "cf11"], ["JB"])
+
+    def targets():
+        cp(T.HF[:], T.HP[:], ["HP"], ["HF"])
+        ts(T.CAPB[:], T.CP[:], -127.5, -256.0, A_.add, A_.mult, ["CP"], ["CAPB"])
+        ts(T.THF[:], T.TH[:], cf(8), cf(9), A_.mult, A_.add, ["TH", "cf8", "cf9"], ["THF"])
+        tt(T.D1[:], T.HF[:, 16:64], T.HF[:, 0:48], A_.subtract, ["HF"], ["D1"])
+        ts(T.KC[:, 3:64:4], T.HF[:, 0:16], 6.0, None, A_.mult, None, ["HF"], ["KC3"])
+        tt(T.D2[:], T.D1[:, 16:48], T.D1[:, 0:32], A_.subtract, ["D1"], ["D2"])
+        ts(T.KC[:, 2:64:4], T.D1[:, 0:16], 6.0, None, A_.mult, None, ["D1"], ["KC2"])
+        tt(T.KC[:, 0:64:4], T.D2[:, 16:32], T.D2[:, 0:16], A_.subtract, ["D2"], ["KC0"])
+        ts(T.KC[:, 1:64:4], T.D2[:, 0:16], 3.0, None, A_.mult, None, ["D2"], ["KC1"])
 
     mwin = T.mm[:, 0:V]
+    HIGH = 9.0 / 16
 
-    def lanes(buf, t): return buf[:, t % Q:V:Q]
+    def keys(name, lo, hi, step=1): return ["%s%d" % (name, i) for i in range(lo // step, -(-hi // step))]
+    def xk(lo, hi, a): return T.XK[:, 16 * lo + a:16 * hi:16]
 
-    def offconv(t):
-        cp(T.OFF[:, t * L:(t + 1) * L], T.SU[:, t:V:Q], ["SU"], ["OFF%d" % t])
+    def gather(q, out, src, add, r, w):
+        if q == "A" and add: ac(out, src, AF.Identity, r, w, bias=add)
+        elif q == "A": ac(out, src, AF.Copy, r, w)
+        elif add: ts(out, src, add, None, A_.add, None, r, w)
+        else: cp(out, src, r, w)
 
-    def succ_a(t, c):
-        c0 = (t % Q) * L + 32 * c
-        ac(T.ZA[:, 512 * c:512 * c + 512], mwin.indirect(T.OFF[:, c0:c0 + 32]), AF.Copy, ["mm", "OFF%d" % (t % Q)], ["ZA%d" % c])
+    def at_least(q, out, in_, bound, r, w):
+        if q == "A": ac(out, in_, AF.Sigmoid, r, w, bias=-4096.0 * (bound - 1.0 / 32), scale=4096.0)
+        else: ts(out, in_, bound, None, A_.is_ge, None, r, w)
 
-    def succ_v(t, c):
-        c0 = (t % Q) * L + 128 + 32 * c
-        sl = slice(512 * c, 512 * c + 512)
-        tt(T.Z[:, sl], mwin.indirect(T.OFF[:, c0:c0 + 32]), T.ZA[:, sl], A_.max, ["mm", "OFF%d" % (t % Q), "ZA%d" % c], ["Z%d" % c])
-
-    def ge8(t):
-        ac(T.GE8[:], lanes(T.mm, t), AF.Sigmoid, ["mm"], ["GE8"], bias=-1920.0, scale=256.0)
-
-    def scan():
-        op("V", lambda: vec.tensor_tensor_scan(T.Z2[:], T.ZM[:], T.Z[:], 0.0, A_.min, A_.max), ["ZM", "Z0", "Z1", "Z2", "Z3"], ["ZS"])
-
-    def g4():
-        for l2 in range(2):
-            ac(B[7][:, L + 128 * l2:L + 128 * l2 + 128], T.Z2[:, 7 + 8 * l2:2048:16], AF.Identity, ["ZS"], ["BM"], ["B7"], bias=-4.0)
-
-    def gx(q, t, lo, hi):
-        end = H + W if t == 0 else 2 * H
-        r = ["XTa", "XTb", "XTc", "LST"] + ([] if t == 0 else ["XTd"])
-        src = T.XT[:, 0:end].indirect(T.LST[:, lo:hi])
-        out = T.XK[:, 16 * lo:16 * hi]
-        keys = ["XK%d" % i for i in range(lo // 32, hi // 32)]
-        if q == "V": cp(out, src, r, keys)
-        else: ac(out, src, AF.Copy, r, keys)
-
-    def xk(c, a): return T.XK[:, 1024 * c + a:1024 * c + 1024:16]
-
-    def pe_sum(c):
-        for a in range(16):
-            mm(B[4][:, 64 * c:64 * c + 64], (T.IDS if a & 1 else T.ID)[:], xk(c, a), a == 0, a == 15,
-               ["XK%d" % (2 * c), "XK%d" % (2 * c + 1), "ID", "IDS"], ["S%d" % c], ["B4"])
-
-    def pe_pack(cs, qs):
-        for q in qs:
-            for c in cs:
-                o = B[q // 2][:, (q % 2) * L + 64 * c:(q % 2) * L + 64 * c + 64]
-                for e in range(2):
-                    mm(o, T.ID[:], xk(c, 2 * q + e), e == 0, e == 1, ["XK%d" % (2 * c), "XK%d" % (2 * c + 1), "ID"],
-                       ["PK%d_%d" % (q, c)], ["B%d" % (q // 2)], sig=(e == 1 and q % 2 == 1 and c == cs[-1]))
-
-    def gs(t, c):
-        if t == 0:
-            src, r = T.ST[:, 0:W].indirect(T.LS0[:, 64 * c:64 * c + 64]), ["STa", "LS0"]
-        else:
-            src, r = T.ST[:].indirect(T.LST[:, 64 * c:64 * c + 64]), ["STa", "STb", "LST"]
-        ac(T.SK[:, 1024 * c:1024 * c + 1024], src, AF.Copy, r, ["SK%d" % c])
-
-    def tr(c):
-        sl = slice(1024 * c, 1024 * c + 1024)
-        op("V", lambda: vec.transpose(T.TR[:, sl], T.SK[:, sl]), ["SK%d" % c], ["TR%d" % c])
-
-    SKEYS = ["S%d" % c for c in range(4)]
-    TRK = ["TR%d" % c for c in range(4)]
-
-    def prod(q):
-        tt(T.PR[:, q * L:(q + 1) * L], B[q // 2][:, (q % 2) * L:(q % 2 + 1) * L], T.OV[:], A_.mult,
-           ["PK%d_%d" % (q, c) for c in range(4)] + ["OV"], ["PR%d" % q], ["B%d" % (q // 2)])
-        if q == 0:
-            mm(B[4][:, L:2 * L], T.COR[:], T.OV[:], True, False, ["COR", "OV"], ["TT"], ["B4"])
-        mm(B[4][:, L:2 * L], T.LW[:, 16 - 2 * q:144 - 2 * q], T.PR[:, q * L:(q + 1) * L], False, q == 7,
-           ["LW", "PR%d" % q], ["TT"], ["B4"])
-
-    def turn(out, mats, keys, rhs, rkeys, start, stop, wkey, bk, sig=None):
+    def turn(bk, mats, mkeys, rhs, rkeys, stop, wkey):
         for h in range(2):
             for gp in range(2):
                 o = 16 - 16 * (gp - h)
-                mm(out(h), mats[h][:, o:o + 128], rhs(gp), start and gp == 0, stop and gp == 1, rkeys + keys, [wkey(h)], [bk(h)],
-                   sig=None if sig is None else (h == 1 and gp == 1))
+                last = h == 1 and gp == 1
+                mm(B[bk][:, h:128:2], mats[h][:, o:o + 128], rhs(gp), False, stop and last, rkeys + mkeys, [wkey], ["B%d" % bk], sig=last)
 
-    ac(mwin, T.MK[:], AF.Copy, ["MK"], ["mm"])
-    ge8(0)
-    offconv(0)
-    for c in range(4):
-        succ_a(0, c)
-        succ_v(0, c)
-    ts(T.XT[:, H:H + W], T.XT[:, 0:W], -8.0, 256.0, A_.add, A_.mult, ["XTa"], ["XTc"])
-    ac(T.XT[:, W:H], T.XT[:, 0:H - W], AF.Copy, ["XTa"], ["XTb"])
-    scan()
-    g4()
-    ts(T.LST[:], T.PL[:, 0:V:Q], cf(0), None, A_.add, None, ["PL", "cf0"], ["LST"])
-
-    for t in range(RO):
+    def step(t, name, i, q):
         d = cores[(rank + 1 + t % (n - 1)) % n]
         s_ = cores[(rank - 1 - t % (n - 1)) % n]
-        first, final = t == 0, t == RO - 1
-        ml = lanes(T.mm, t)
-        for c in range(3):
-            gx("A", t, 64 * c, 64 * c + 32)
-            gx("V", t, 64 * c + 32, 64 * c + 64)
-            pe_sum(c)
-            pe_pack([c], range(8 if c < 2 else 4))
-        if first:
-            gx("A", t, 192, 224)
-            gx("V", t, 224, 256)
-            cp(T.LS0[:], T.PL[:, 0:V:Q], ["PL"], ["LS0"])
-            cp(T.pp[:, 0:V], T.PL[:], ["PL"], ["pp"])
-        else:
-            gx("A", t, 192, 256)
-            for c in range(N1, 4): succ_v(t, c)
-            scan()
-        pe_sum(3)
-        pe_pack([3], range(4))
-        pe_pack([2, 3], range(4, 8))
-        ac(T.OV[:], B[4][:, 0:L], AF.Sigmoid, SKEYS + ["BIAS", "CAPB"], ["OV"], ["B4"],
-           bias=(T.CAPB if first else T.BIAS)[:], scale=256.0)
-        ac(T.SB[:], B[4][:, 0:L], AF.Identity, SKEYS, ["SB"], ["B4"], bias=64.0)
-        if not first: g4()
-        for c in range(4): gs(t, c)
-        for p in range(16):
-            mm(B[5][:, 0:16], T.WN[:, 16 - p:144 - p], T.SB[:, p:L:16], p == 0, p == 15, ["WN", "SB"], ["UP"], ["B5"])
-        for q in range(4): prod(q)
-        cp(T.U[:, 0:16], B[5][:, 0:16], ["UP"], ["U"], ["B5"])
-        for r_ in range(16):
-            sh = 16 * (r_ & 1) + 2 * (r_ >> 1)
-            mm(B[5][:, 16:32], T.WS[:, 32 - sh:160 - sh], T.SB[:, r_:L:16], r_ == 0, r_ == 15, ["WS", "SB"], ["UQ"], ["B5"])
-        prod(4)
-        ts(T.BB[:], T.U[:, 0:16], 4, 3, A_.logical_shift_right, A_.bitwise_and, ["U"], ["BB"])
-        prod(5)
-        for i, key in ((1, "D0a"), (2, "D0b"), (3, "D0c")):
-            ts(T.D0[:, i:64:4], T.BB[:], float(i - 3), None, A_.add, None, ["BB"], [key])
-        op("V", lambda: vec.tensor_tensor_scan(T.C6[:], T.D0[:], T.KC[:], 0.0, A_.mult, A_.add),
-           ["D0a", "D0b", "D0c", "KC0", "KC1", "KC2", "KC3"], ["C6"])
-        prod(6)
-        ts(T.cS[:, 16 * t:16 * t + 16], T.C6[:, 3:64:4], 1.0 / 6, 0.25, A_.mult, A_.add, ["C6"], ["cS%d" % t])
-        send("c", t, d, 16)
-        prod(7)
-        cp(T.U[:, 16:32], B[5][:, 16:32], ["UQ"], ["U2"], ["B5"])
-        tt(T.NEWA[:], B[7][:, L:2 * L], ml, A_.max, ["BM", "mm"], ["NEWA"], ["B7"])
-        mm(B[5][:, 32:48], T.ID6[:], T.DUM[:], True, False, ["ID6", "DUM"], ["OL"], ["B5"])
-        for p in range(16):
-            mm(B[5][:, 32:48], T.BP[:, 16 - p:144 - p], T.GE8[:, p:L:16], False, False, ["BP", "GE8"], ["OL"], ["B5"])
-        mm(B[6][:, 0:L], T.BON[:], T.GE8[:], True, False, ["BON", "GE8"], ["CN"], ["B6"], sig=True)
-        mm(B[1][:, 0:L], T.ID32[:], lanes(T.pp, t), True, False, ["ID32", "pp"], ["X"], ["B1"], sig=True)
-        cp(T.TI[:], B[4][:, L:2 * L], ["TT"], ["TI"], ["B4"])
-        ts(T.J1[:], T.U[:, 16:32], 15, None, A_.bitwise_and, None, ["U2"], ["J1"])
-        ts(T.LI[:], T.TI[:], 8, 255, A_.logical_shift_right, A_.bitwise_and, ["TI"], ["LI"])
-        ts(T.J2[:], T.J1[:], 1.0, cf(11), A_.max, A_.add, ["J1", "cf11"], ["J2"])
-        ts(B[7][:, 0:L], T.LI[:], T.THF[:, t:t + 1], 15.0, A_.is_ge, A_.mult, ["LI", "THF"], ["F15"], ["B7"])
-        tt(T.J3[:], T.J2[:], T.JB[:], A_.add, ["J2", "JB"], ["J3"])
-        tt(ml, B[7][:, 0:L], T.NEWA[:], A_.max, ["F15", "NEWA"], ["mm"], ["B7"])
-        cp(T.JL[:], T.J3[:], ["J3"], ["JL"])
-        ts(T.HI[:], ml, 8.0, None, A_.is_ge, None, ["mm"], ["HI"])
-        for p in range(16):
-            mm(B[5][:, 32:48], T.BN[:, 16 - p:144 - p], T.HI[:, p:L:16], False, p == 15, ["BN", "HI"], ["OL"], ["B5"])
-        mm(B[6][:, 0:L], T.BOP[:], T.HI[:], False, True, ["BOP", "HI"], ["CN"], ["B6"])
-
-        def back():
-            ts(T.bS[:, t * L:(t + 1) * L], mwin.indirect(T.cR[:, 16 * t:16 * t + 16]), -4.0, None, A_.add, None,
-               ["mm", "cR%d" % t], ["bS%d" % t])
-            send("b", t, s_, L)
-
-        if final: tr(0)
-        else: back()
-        tt(T.L6[:], B[5][:, 32:48], T.C6[:, 3:64:4], A_.max, ["OL", "C6"], ["L6"], ["B5"])
-        ts(T.lS[:, 16 * t:16 * t + 16], T.L6[:], 1.0 / 6, 0.25, A_.mult, A_.add, ["L6"], ["lS%d" % t])
-        send("l", t, d, 16)
-        if not final: tr(0)
-        if not final:
-            ac(T.JK[:], B[6][:, 0:L], AF.Sigmoid, ["CN"], ["JK", "AC"], ["B6"], bias=-128.0, scale=256.0, accum_out=T.AC[:])
-        tr(1)
-        tr(2)
-        ac(T.SJ[:, 0:192], T.TR[:, 0:3072].indirect(T.JL[:, 0:12]), AF.Copy, TRK[:3] + ["JL"], ["SJ"])
-        tr(3)
-        ac(T.SJ[:, 192:L], T.TR[:].indirect(T.JL[:, 12:16]), AF.Copy, TRK + ["JL"], ["SJ"])
-        turn(lambda h: B[2 * h][:, 0:128], (T.I0N, T.I1N), ["I0N", "I1N"], lambda gp: T.TR[:, 16 * gp:4096:32], TRK,
-             True, False, lambda h: "DD%d" % h, lambda h: "B%d" % (2 * h))
-        turn(lambda h: B[2 * h][:, 0:128], (T.I0P, T.I1P), ["I0P", "I1P"], lambda gp: T.SJ[:, gp:L:2], ["SJ"],
-             False, True, lambda h: "DD%d" % h, lambda h: "B%d" % (2 * h))
-        turn(lambda h: B[1][:, h:L:2], (T.I0P, T.I1P), ["I0P", "I1P"], lambda gp: T.TR[:, 16 * gp:4096:32], TRK,
-             False, False, lambda h: "X", lambda h: "B1", sig=True)
-        if not final:
-            cp(T.AI[:], T.AC[:], ["AC"], ["AI"])
-            if first:
-                ts(T.XT[:, H + W:2 * H], T.XT[:, H:2 * H - W], 1.0, None, A_.mult, None, ["XTc"], ["XTd"])
-            if t + 1 < Q: offconv(t + 1)
+        first, final, cl = t == 0, t == RO - 1, t % Q
+        ml, end = T.mm[:, cl:V:Q], W if first else H
+        c16, c256 = slice(16 * t, 16 * t + 16), slice(L * t, L * t + L)
+        half = slice(128 * i, 128 * i + 128) if i is not None else None
+        if name == "levels" and q == "A": ac(mwin, T.MK[:], AF.Identity, ["MK"], ["mm"], bias=1.0 / 16, scale=1.0 / 16)
+        if name == "levels" and q == "V": ts(mwin, T.MK[:], 1.0, 1.0 / 16, A_.add, A_.mult, ["MK"], ["mm"])
+        if name == "places": cp(T.pp[:, 0:V], T.PL[:], ["PL0", "PL1"], ["pp"])
+        if name == "targets": targets()
+        if name == "own": cp(T.WF[:], T.PL[:, 0:V:Q], ["PL0", "PL1"], ["WF0", "WF1"])
+        if name == "list" and first:
+            lo, hi = (0, 64) if i == 0 else (64, L)
+            cp(T.LST[:, lo:hi], T.PL[:, Q * lo:Q * hi:Q], ["PL%d" % i], ["LST%d" % i])
+        if name == "list" and not first: cp(T.LST[:], T.pp[:, cl:V:Q], ["pp"], ["LST0", "LST1"])
+        if name == "off" and i is not None: cp(T.OFF[:, half], T.SU[:, 640 * i:640 * i + 640:Q], ["SU%d" % i], ["OFF0_%d" % i])
+        if name == "off" and i is None and t + 1 < Q:
+            cp(T.OFF[:, L * t + L:L * t + 2 * L], T.SU[:, t + 1:V:Q], ["SU0", "SU1"], keys("OFF%d_" % (t + 1), 0, 2))
+        if name in ("za", "zv"):
+            h = int(name == "zv")
+            c0, sl = cl * L + 128 * h + 32 * i, slice(512 * i, 512 * i + 512)
+            src, r = mwin.indirect(T.OFF[:, c0:c0 + 32]), ["mm", "OFF%d_%d" % (cl, h)]
+            if h: tt(T.Z[:, sl], src, T.ZA[:, sl], A_.max, r + ["ZA%d" % i], ["Z%d" % i])
+            else: gather(q, T.ZA[:, sl], src, 0, r, ["ZA%d" % i])
+        if name == "scan":
+            op("V", lambda: vec.tensor_tensor_scan(T.Z2[:], T.ZM[:], T.Z[:], 0.0, A_.min, A_.max), ["ZM"] + keys("Z", 0, 4), ["ZS"])
+        if name == "g4":
+            mm(pG, T.IDM4[:], T.ONE[:], True, False, ["IDM4", "ONE"], ["G"] + keys("S", 0, 4), ["B4"])
+            for l in range(2):
+                mm(B[4][:, 128 * l:128 * l + 128], T.ID[:], T.Z2[:, 8 * l + 7:2048:16], False, l == 1, ["ID", "ZS"], ["G"], ["B4"])
+        if name == "newa": tt(T.NEWA[:], pG, ml, A_.max, ["G", "mm"], ["NEWA"], ["B4"])
+        if name == "ge8": at_least(q, T.GE8[:], ml, HIGH, ["mm"], ["GE8"])
+        if name == "olg":
+            mm(pOL, T.ID6[:], T.DUM[:], True, False, ["ID6", "DUM"], ["OL"], ["B5"])
+            for p in range(16):
+                mm(pOL, T.BP[:, 16 - p:144 - p], T.GE8[:, p:L:16], False, False, ["BP", "GE8"], ["OL"], ["B5"], sig=p == 15)
+        if name == "x":
+            gather(q, T.XK[:, 512 * i:512 * i + 512], T.XT[:, 0:end].indirect(T.LST[:, 32 * i:32 * i + 32]), -8.0,
+                   ["XTa", "LST%d" % min(i // 2, 1)] + ([] if first else ["XTb"]), ["XK%d" % i])
+        if name == "sum":
+            for a in range(16):
+                mm(B[4][:, 64 * i:64 * i + 64], T.ID[:], xk(64 * i, 64 * i + 64, a), a == 0, a == 15,
+                   keys("XK", 2 * i, 2 * i + 2) + ["ID"], ["S%d" % i, "BM"], ["B4"])
+        if name == "pack":
+            lo, qs = ((0, range(8)), (128, range(4)), (128, range(4, 8)))[i]
+            for p in qs:
+                if p >= PAIRS: continue
+                o = B[p // 2][:, (p % 2) * L + lo:(p % 2) * L + lo + 128]
+                for e in range(2):
+                    mm(o, (T.IDK if e else T.ID)[:], xk(lo, lo + 128, 2 * p + e), e == 0, e == 1, keys("XK", lo, lo + 128, 32) + ["ID", "IDK"],
+                       ["PK%d_%d" % (p, lo // 128), ("X%d" if p & 2 else "DD%d") % (p // 4)], ["B%d" % (p // 2)])
+        if name == "ov":
+            ac(T.OV[:], pS, AF.Sigmoid, keys("S", 0, 4) + ["BIAS", "CAPB"], ["OV"], ["B4"], bias=(T.CAPB if first else T.BIAS)[:], scale=256.0)
+        if name == "sb": ac(T.SB[:], pS, AF.Identity, keys("S", 0, 4), ["SB"], ["B4"], bias=128.0)
+        if name == "pr":
+            tt(T.PR[:, i * L:(i + 1) * L], B[i // 2][:, (i % 2) * L:(i % 2 + 1) * L], T.OV[:], A_.mult,
+               keys("PK%d_" % i, 0, 2) + ["OV"], ["PR%d" % i], ["B%d" % (i // 2)])
+        if name == "t":
+            if i == 0: mm(pT, T.COR[:], T.OV[:], True, False, ["COR", "OV"], ["TT", "CN"], ["B6"])
+            if i < PAIRS:
+                mm(pT, T.LW[:, 16 - 2 * i:144 - 2 * i], T.PR[:, i * L:(i + 1) * L], False, i == 7, ["LW", "PR%d" % i], ["TT"], ["B6"], sig=True)
+            else:
+                for e in range(2):
+                    c0 = 512 * (i - 6) + L * e
+                    mm(pT, (T.LWK if e else T.LW1)[:, 16 - 2 * i:144 - 2 * i], T.RL[:, c0:c0 + L], False, i == 7 and e == 1,
+                       ["LW1", "LWK", "RL%d" % i], ["TT"], ["B6"], sig=e == 1)
+        if name == "pa":
+            bk = 7 if i == 7 else 3
+            for e in range(2):
+                o, w = B[bk][:, L * e:L * e + L], ["PA%d" % i] + (["F15"] if i == 7 else ["X1", "PK6_0"])
+                mm(o, T.ID16[:], T.OV[:], True, False, ["ID16", "OV"], w, ["B%d" % bk])
+                mm(o, T.ID[:], xk(0, L, 2 * i + e), False, True, keys("XK", 0, 8) + ["ID"], w, ["B%d" % bk], sig=e == 1)
+        if name == "ra":
+            bk = 7 if i == 7 else 3
+            ac(T.RL[:, 512 * (i - 6):512 * (i - 5)], B[bk][:], AF.Relu, ["PA%d" % i] + ([] if i == 7 else ["PK6_0"]), ["RL%d" % i], ["B%d" % bk], bias=-8.0)
+        if name == "na": at_least(q, T.NA8[:], T.NEWA[:], HIGH, ["NEWA"], ["NA8"])
+        if name == "hf": tt(T.HI[:], pF, T.NA8[:], A_.max, ["F15", "NA8"], ["HI"], ["B7"])
+        if name == "rq" and q == "A": ac(T.RQ[:], pT, AF.Identity, ["TT"], ["RQ"], ["B6"], bias=1280.0 - 120.0 / PK, scale=1.0 / PK)
+        if name == "rq" and q == "V": ts(T.RQ[:], pT, 1.0 / PK, 1280.0 - 120.0 / PK, A_.mult, A_.add, ["TT"], ["RQ"], ["B6"])
+        if name == "r2": ac(T.R2[:], T.RQ[:], AF.Identity, ["RQ", "THF", "cf0"], ["R2"], bias=T.THF[:, t:t + 1], scale=cf(0))
+        if name == "f": tt(pF, pT, T.R2[:], A_.is_ge, ["TT", "R2"], ["F15", "PA7"], ["B6", "B7"])
+        if name == "ml": tt(ml, pF, T.NEWA[:], A_.max, ["F15", "NEWA"], ["mm"], ["B7"])
+        if name == "hi": at_least(q, T.HI[:], ml, HIGH, ["mm"], ["HI"])
+        if name == "pu":
+            for p in range(16):
+                mm(pU, T.WN[:, 16 - p:144 - p], T.SB[:, p:L:16], p == 0, p == 15, ["WN", "SB"], ["UP"], ["B4"])
+        if name == "u": cp(T.U[:], pU, ["UP"], ["U"], ["B4"])
+        if name == "bb": ts(T.BB[:], T.U[:], 4, 3, A_.logical_shift_right, A_.bitwise_and, ["U"], ["BB"])
+        if name == "d":
+            for k in range(1, 4): ts(T.D0[:, k:64:4], T.BB[:], float(k - 3), None, A_.add, None, ["BB", "D0"], ["D0%d" % k])
+        if name == "c":
+            op("V", lambda: vec.tensor_tensor_scan(T.C6[:], T.D0[:], T.KC[:], 0.0, A_.mult, A_.add), keys("D0", 1, 4) + keys("KC", 0, 4), ["C6"])
+        if name == "cs": ts(T.cS[:, c16], T.C6[:, 3:64:4], 1.0 / 6, 0.25, A_.mult, A_.add, ["C6"], ["cS"])
+        if name == "j" and i == 1: ts(T.J1[:], T.U[:], 15, None, A_.bitwise_and, None, ["U"], ["J1"])
+        if name == "j" and i == 2: ts(T.J2[:], T.J1[:], 1.0, None, A_.max, None, ["J1"], ["J2"])
+        if name == "pj":
+            mm(pJ, T.IDH[:], T.JB[:], True, False, ["IDH", "JB"], ["JP"], ["B4"])
+            mm(pJ, T.PERM[:], T.J2[:], False, True, ["PERM", "J2"], ["JP"], ["B4"])
+        if name == "jl": cp(T.JL[:], pJ, ["JP"], ["JL"], ["B4"])
+        if name == "ol":
+            for p in range(16):
+                mm(pOL, T.BN[:, 16 - p:144 - p], T.HI[:, p:L:16], False, p == 15, ["BN", "HI"], ["OL"], ["B5"])
+        if name == "cn":
+            mm(pCN, T.BON[:], T.GE8[:], True, False, ["BON", "GE8"], ["CN"], ["B6"])
+            mm(pCN, T.BOP[:], T.HI[:], False, True, ["BOP", "HI"], ["CN"], ["B6"])
+        if name == "l": tt(T.L6[:], pOL, T.C6[:, 3:64:4], A_.max, ["OL", "C6"], ["L6"], ["B5"])
+        if name == "ls": ts(T.lS[:, c16], T.L6[:], 1.0 / 6, 0.25, A_.mult, A_.add, ["L6"], ["lS"])
+        if name == "jk" and final: ac(T.JK[:], pCN, AF.Sigmoid, ["CN"], ["JK"], ["B6"], bias=-128.0, scale=256.0)
+        if name == "jk" and not final:
+            ac(T.JK[:], pCN, AF.Sigmoid, ["CN"], ["JK", "AC"], ["B6"], bias=-128.0, scale=256.0, accum_out=T.AC[:])
+        if name == "ai": cp(T.AI[:], T.AC[:], ["AC"], ["AI"])
+        if name == "a":
             ts(T.A7[:], T.AI[:], 7, None, A_.bitwise_and, None, ["AI"], ["A7"])
             ts(T.BIAS[:], T.A7[:], -256.0, T.CAPB[:], A_.mult, A_.add, ["A7", "CAPB"], ["BIAS"])
-        else:
-            back()
-            ac(T.FL[:], T.pp[:, 0:V], AF.Sigmoid, ["pp"], ["FL"], bias=-256.0 * (W - 0.5), scale=256.0)
-        for h in range(2):
-            tt(T.HD[:, h:L:2], B[2 * h][:, 0:128], T.HI[:, h:L:2], A_.mult, ["DD%d" % h, "HI"], ["HD%d" % h], ["B%d" % (2 * h)])
-        mm(B[1][:, 0:L], T.ID[:], T.HD[:], False, True, ["ID", "HD0", "HD1"], ["X"], ["B1"])
-        ks = T.kS[:, t * L:(t + 1) * L]
-        if not final:
-            cp(ks, B[1][:, 0:L], ["X"], ["kS%d" % t], ["B1"])
-        else:
-            ts(T.WF[:], B[1][:, 0:L], float(W), float(W), A_.is_ge, A_.mult, ["X"], ["WF"], ["B1"])
-            tt(T.WY[:], B[1][:, 0:L], T.WF[:], A_.subtract, ["X", "WF"], ["WY"], ["B1"])
-            cp(ks, T.WY[:], ["WY"], ["kS%d" % t])
-        send("k", t, d, L)
-        ac(T.mm[:].indirect(T.lR[:, 16 * t:16 * t + 16]), T.NEG[:], AF.Sigmoid, ["NEG", "lR%d" % t], ["mm"])
-        if final:
-            pieces = [(3, 0, 512), (4, 512, 1024), (5, 1024, V)]
-            for bk, lo, hi_ in pieces:
-                ac(B[bk][:, 0:hi_ - lo], T.FL[:, lo:hi_], AF.Copy, ["FL"], ["NF%d" % bk], ["B%d" % bk], scale=-float(W))
-        tt(B[7][:, L:2 * L], B[6][:, 0:L], T.bR[:, t * L:(t + 1) * L], A_.min, ["CN", "bR%d" % t], ["BM"], ["B6", "B7"])
-        tt(ml, B[7][:, L:2 * L], ml, A_.max, ["BM", "mm"], ["mm"], ["B7"])
-        if not final:
-            for c in range(4): succ_a(t + 1, c)
-            ge8(t + 1)
-            for c in range(N1): succ_v(t + 1, c)
-        else:
-            ac(T.MK[:], mwin, AF.Copy, ["mm"], ["MK"])
+        if name == "s":
+            gather(q, T.SK[:, 512 * i:512 * i + 512], T.ST[:, 0:end].indirect(T.LST[:, 32 * i:32 * i + 32]), 0,
+                   ["STa", "LST%d" % min(i // 2, 1)] + ([] if first else ["STb"]), ["SK%d" % i])
+        if name == "tr":
+            sl = slice(1024 * i, 1024 * i + 1024)
+            op("V", lambda: vec.transpose(T.TR[:, sl], T.SK[:, sl]), keys("SK", 2 * i, 2 * i + 2), ["TR%d" % i])
+        if name == "open":
+            for z in range(2):
+                src, key = (T.WF[:, 128 * z:128 * z + 128], "WF%d" % z) if first else (T.pp[:, cl + 640 * z:640 * z + 640:Q], "pp")
+                mm(B[2 * z][:, 0:128], T.ID0[:], T.ONE[:, 0:128], True, False, ["ID0", "ONE"],
+                   ["DD%d" % z] + keys("PK%d_" % (4 * z), 0, 2) + keys("PK%d_" % (4 * z + 1), 0, 2), ["B%d" % (2 * z)])
+                mm(B[2 * z + 1][:, 0:128], T.ID32[:], src, True, False, ["ID32", key],
+                   ["X%d" % z] + keys("PK%d_" % (4 * z + 2), 0, 2) + keys("PK%d_" % (4 * z + 3), 0, 2), ["B%d" % (2 * z + 1)], sig=True)
+        if name == "pick":
+            gather("A", T.SJ[:, half], T.TR[:, 0:2048 * i + 2048].indirect(T.JL[:, 8 * i:8 * i + 8]), 0, keys("TR", 0, 2 * i + 2) + ["JL"], ["SJ%d" % i])
+        if name == "turn":
+            trk, move0 = keys("TR", 2 * i, 2 * i + 2), lambda gp: T.TR[:, 2048 * i + 16 * gp:2048 * i + 2048:32]
+            turn(2 * i, (T.I0N, T.I1N), ["I0N", "I1N"], move0, trk, False, "DD%d" % i)
+            turn(2 * i, (T.I0P, T.I1P), ["I0P", "I1P"], lambda gp: T.SJ[:, 128 * i + gp:128 * i + 128:2], ["SJ%d" % i], True, "DD%d" % i)
+            turn(2 * i + 1, (T.I0P, T.I1P), ["I0P", "I1P"], move0, trk, False, "X%d" % i)
+        if name == "hd": tt(T.HD[:, half], B[2 * i][:, 0:128], T.HI[:, half], A_.mult, ["DD%d" % i, "HI"], ["HD%d" % i], ["B%d" % (2 * i)])
+        if name == "xs": mm(B[2 * i + 1][:, 0:128], T.ID[:], T.HD[:, half], False, True, ["ID", "HD%d" % i], ["X%d" % i], ["B%d" % (2 * i + 1)])
+        if name == "ks":
+            out, x, bk = T.kS[:, L * t + 128 * i:L * t + 128 * i + 128], B[2 * i + 1][:, 0:128], ["B%d" % (2 * i + 1)]
+            if not final:
+                cp(out, x, ["X%d" % i], ["kS%d" % i], bk)
+            else:
+                ts(T.WF[:, half], x, float(W), float(W), A_.is_ge, A_.mult, ["X%d" % i], ["WF%d" % i], bk)
+                tt(T.WY[:, half], x, T.WF[:, half], A_.subtract, ["X%d" % i, "WF%d" % i], ["WY%d" % i], bk)
+                cp(out, T.WY[:, half], ["WY%d" % i], ["kS%d" % i])
+        if name == "sendc": send("c", "rc%d" % t, d, 16 * t, 16 * t + 16, ["cS"])
+        if name == "sendl": send("l", "rl%d" % t, d, 16 * t, 16 * t + 16, ["lS"])
+        if name == "sendb": send("b", "rb%d" % t, s_, L * t, L * t + L, ["bS"])
+        if name == "sendk" and i is None: send("k", "rk%d" % t, d, L * t, L * t + L, ["kS0", "kS1"])
+        if name == "sendk" and i is not None: send("k", "r%s%d" % ("kj"[i], t), d, L * t + 128 * i, L * t + 128 * i + 128, ["kS%d" % i])
+        if name == "back": gather(q, T.bS[:, c256], mwin.indirect(T.cR[:, c16]), -1.25, ["mm", "rc%d" % t], ["bS"])
+        if name == "zero": ac(T.mm[:].indirect(T.lR[:, c16]), T.NEG[:], AF.Sigmoid, ["NEG", "rl%d" % t], ["mm"])
+        if name == "bm":
+            mm(pBM, T.ID[:], T.JK[:], True, False, ["ID", "JK"], ["BM", "G"], ["B4"])
+            mm(pBM, T.ID[:], T.bR[:, c256], False, True, ["ID", "rb%d" % t], ["BM"], ["B4"])
+        if name == "step": tt(ml, pBM, ml, A_.max, ["BM", "mm"], ["mm"], ["B4"])
+        if name in ("land", "prev"):
+            u = t if name == "land" and i is not None else t - 1
+            lo, w = (0, 16) if i is None else (8 * i, 8)
+            cp(T.pp[:].indirect(T.lR[:, 16 * u + lo:16 * u + lo + w]), T.kR[:, L * u + 16 * lo:L * u + 16 * (lo + w)],
+               ["rl%d" % u, "r%s%d" % ("kj"[i or 0], u)], ["pp"] + keys("pp", 0, 3))
+        if name == "wrap":
+            bk, lo, hi = ((0, 0, 512), (2, 512, 1024), (7, 1024, V))[i]
+            ts(B[bk][:, 0:hi - lo], T.pp[:, lo:hi], float(W), -float(W), A_.is_ge, A_.mult, ["pp"], [("DD0", "DD1", "F15")[i]], ["B%d" % bk])
+            tt(T.pp[:, lo:hi], B[bk][:, 0:hi - lo], T.pp[:, lo:hi], A_.add, [("DD0", "DD1", "F15")[i], "pp", "X0", "X1"], ["pp%d" % i], ["B%d" % bk])
+        if name == "outm":
+            ac(T.MK[:], mwin, AF.Relu, ["mm"], ["MK"], bias=-1.0, scale=16.0)
             dmas("ymk", [("S", T.ymk[:], T.MK[:])], r=["MK"])
-            for bk, lo, hi_ in pieces:
-                tt(T.pp[:, lo:hi_], B[bk][:, 0:hi_ - lo], T.pp[:, lo:hi_], A_.add, ["NF%d" % bk, "pp"], ["pp%d" % bk], ["B%d" % bk])
-        cp(T.pp[:].indirect(T.lR[:, 16 * t:16 * t + 16]), T.kR[:, t * L:(t + 1) * L], ["lR%d" % t, "kR%d" % t],
-           ["pp"] + (["pp3", "pp4", "pp5"] if final else []))
-        if not final:
-            ts(T.LST[:], lanes(T.pp, t + 1), cf(0), None, A_.add, None, ["pp", "cf0"], ["LST"])
-    dmas("ypl", [("S", T.ypl[:], T.pp[:, 0:V])], r=["pp"])
+        if name == "outp": dmas("ypl", [("S", T.ypl[:], T.pp[:, 0:V])], r=["pp"])
+
+    for t in range(RO):
+        for word in (FIRST if t == 0 else LAST if t == RO - 1 else MIDDLE).split():
+            name, q = (word + ":").split(":")[:2]
+            if name[-1].isdigit() and name != "ge8" and name != "g4" and name != "r2": step(t, name[:-1], int(name[-1]), q)
+            else: step(t, name, None, q)
     for s, v in total.items():
         if known["G"].get(s, 0) < v:
             g.wait_ge(T.sem[s], v)

from concourse.bass import DstId, RemoteDMATransfer
from concourse.mybir import dt, AluOpType, AxisListType, ActivationFunctionType

W, V, Q, L, RO = 2816, 1280, 5, 256, 6
H = 4096
PK = 241
BIG = 16384.0
PAIRS = 8

LOADS = "sm pl0 xf pl1 mk su0 su1 st xw"
FIRST = """list0 x0:A x1:V targets list1 sum0 x2:A x3:V sum1 x4:A x5:V x6:A x7:V levels:A sum2 sum3 pack0 ov ge8:A sb own off0
za0:A za1:A za2:A za3:V off1 s0:A s1:A s2:A s3:A s4:A pack1 pr0 pr1 pr2 pr3 pu u pack2 bb d0 c6 cs sendc pr4 pr5 pr6 pr7 j1 j2
zv0 zv1 zv2 zv3 t0 t1 t2 t3 t4 open olg pj t5 t6 t7 jl scan g4 rq:A r2 s5:A s6:A s7:A tr0 newa f na8:V hf ol tr1 ml back:A pick0 cn
turn0 l6 ls sendl sendb tr2 tr3 hd0 jk pick1 off ai xs0 ks0 turn1 hd1 xs1 a7 ks1 sendk places zero bm step4"""
FRONT = """za0:V za1:A ge8:A za2:A za3:A olg zv0 land list x0:A x1:V sum0 x2:A x3:V sum1 pack0 x4:A x5:V sum2 x6:A x7:A sum3
zv1 zv2 zv3 s0:A ov sb scan pack1 pr0 pr1 pr2 pr3 s1:A s2:A s3:A s4:A pu u bb j1 pack2 t0 t1 g4 d0 j2 pr4 c6 pr5 cs sendc pr6
t2 t3 t4 t5 t6 pr7 t7 pj tr0 newa na8:V rq:A r2 f """
MIDDLE = FRONT + """hf tr1 ml ol cn open l6 jl ls sendl back:V sendb s5:A s6:A s7:A pick0 jk turn0 tr2 tr3 hd0 ai off a7
pick1 turn1 hd1 xs0 ks0 xs1 ks1 sendk zero bm step4"""
LAST = FRONT + """open jl hf ol tr1 ml cn l6 s5:A s6:A pick0 s7:A ls back:A turn0 tr2 hd0 sendl tr3 sendb pick1 jk zero xs0 turn1
ks0 hd1 sendk0 xs1 ks1 sendk1 bm wrap0 step4 wrap1 wrap2 outm land0 land1 outp"""

F32, BF, F16, I32, U16 = "float32", "bfloat16", "float16", "int32", "uint16"
SCRATCH = {
    "XT": ("sbuf", [128, H], BF), "ST": ("sbuf", [128, H], BF),
    "XK": ("sbuf", [128, 4096], BF), "SK": ("sbuf", [128, 4096], BF), "TR": ("sbuf", [128, 4096], BF),
    "PR": ("sbuf", [128, 2048], F16),
    "pp": ("sbuf", [128, V + L], F32), "mm": ("sbuf", [128, V + L], F32),
    "PL": ("sbuf", [128, V], I32), "SU": ("sbuf", [128, V], I32), "MK": ("sbuf", [128, V], BF),
    "OFF": ("sbuf", [128, V], U16), "LST": ("sbuf", [128, L], U16),
    "ZA": ("sbuf", [128, 2048], BF), "Z": ("sbuf", [128, 2048], BF), "Z2": ("sbuf", [128, 2048], BF), "ZM": ("sbuf", [128, 2048], BF),
    "GE8": ("sbuf", [128, L], BF), "NEWA": ("sbuf", [128, L], BF), "HI": ("sbuf", [128, L], BF),
    "OV": ("sbuf", [128, L], BF), "SB": ("sbuf", [128, L], BF), "SJ": ("sbuf", [128, L], BF), "HD": ("sbuf", [128, L], BF),
    "JK": ("sbuf", [128, L], BF), "NEG": ("sbuf", [128, L], F32), "RQ": ("sbuf", [128, L], F16), "R2": ("sbuf", [128, L], F32),
    "ONE": ("sbuf", [128, L], BF), "WF": ("sbuf", [128, L], F32), "WY": ("sbuf", [128, L], F32),
    "HP": ("sbuf", [128, 64], I32), "HF": ("sbuf", [128, 64], F32), "D1": ("sbuf", [128, 48], F32), "D2": ("sbuf", [128, 32], F32),
    "KC": ("sbuf", [128, 64], F32), "D0": ("sbuf", [128, 64], F32), "C6": ("sbuf", [128, 64], F32),
    "CP": ("sbuf", [128, 1], I32), "TH": ("sbuf", [128, RO], I32), "THF": ("sbuf", [128, RO], F32),
    "CAPB": ("sbuf", [128, 1], F32), "BIAS": ("sbuf", [128, 1], F32), "AC": ("sbuf", [128, 1], F32),
    "AI": ("sbuf", [128, 1], I32), "A7": ("sbuf", [128, 1], I32),
    "U": ("sbuf", [128, 16], I32), "BB": ("sbuf", [128, 16], I32), "J1": ("sbuf", [128, 16], I32),
    "J2": ("sbuf", [128, 16], F16), "JL": ("sbuf", [128, 16], U16), "L6": ("sbuf", [128, 16], F32),
    "PID": ("sbuf", [128, 1], I32), "CI": ("sbuf", [128, 8], I32), "CF": ("sbuf", [128, 16], F32),
    "NR": ("sbuf", [128, 160], F32), "G16R": ("sbuf", [128, 128], F32),
    "WN": ("sbuf", [128, 160], BF), "BP": ("sbuf", [128, 160], BF), "BN": ("sbuf", [128, 160], BF),
    "LW": ("sbuf", [128, 160], F16), "LA": ("sbuf", [128, 160], F32), "LB": ("sbuf", [128, 160], F32),
    "I0P": ("sbuf", [128, 160], BF), "I1P": ("sbuf", [128, 160], BF), "I0N": ("sbuf", [128, 160], BF), "I1N": ("sbuf", [128, 160], BF),
    "ID": ("sbuf", [128, 128], BF), "IDK": ("sbuf", [128, 128], BF), "ID32": ("sbuf", [128, 128], F32), "ID6": ("sbuf", [128, 128], F16),
    "IDM4": ("sbuf", [128, 128], BF), "ID0": ("sbuf", [128, 128], BF), "ID16": ("sbuf", [128, 128], BF), "AR": ("sbuf", [128, 128], F32),
    "LW1": ("sbuf", [128, 160], BF), "LWK": ("sbuf", [128, 160], BF), "RL": ("sbuf", [128, 1024], BF), "NA8": ("sbuf", [128, L], BF),
    "IDH": ("sbuf", [128, 128], F16), "PERM": ("sbuf", [128, 128], F16),
    "BOP": ("sbuf", [128, 128], BF), "BON": ("sbuf", [128, 128], BF), "BO1": ("sbuf", [128, 128], F32), "COR": ("sbuf", [128, 128], BF),
    "JB": ("sbuf", [128, 16], F16), "DUM": ("sbuf", [128, 16], F16),
    "cS": ("sbuf", [128, RO * 16], U16), "cR": ("sbuf", [128, RO * 16], U16),
    "lS": ("sbuf", [128, RO * 16], U16), "lR": ("sbuf", [128, RO * 16], U16),
    "bS": ("sbuf", [128, RO * L], BF), "bR": ("sbuf", [128, RO * L], BF),
    "kS": ("sbuf", [128, RO * L], U16), "kR": ("sbuf", [128, RO * L], U16),
}
for _b in range(8):
    SCRATCH["B%d" % _b] = ("psum", [128, 512], F32)

DMAS = ["pl0", "pl1", "xf", "mk", "su0", "su1", "sm", "st", "xw", "ypl", "ymk"]
SEMAPHORES = ["cV", "cA", "cP", "cG", "sent"] + ["d_" + n for n in DMAS] + \
             ["r%s%d" % (k, t) for k in "clbkj" for t in range(RO)]


def rank_program(g, core, T, topo):
    rank = T.rank_of(core)
    if rank is None:
        return
    cores = T.cores
    n = len(cores)
    A_ = AluOpType
    AF = ActivationFunctionType
    Qs = {"V": g.vector, "A": g.scalar, "P": g.tensor, "G": g, "S": g.sync}
    cnt = {"cV": 0, "cA": 0, "cP": 0, "cG": 0}
    known = {q: {} for q in Qs}
    lastw, readers, bank = {}, {}, {}
    total = {}

    def wait(q, toks):
        need = {}
        for tk in toks:
            if known[q].get(tk[0], 0) < tk[1] and need.get(tk[0], (0, 0))[1] < tk[1]:
                need[tk[0]] = tk
        for s, tk in need.items():
            if not any(o[0] != s and o[2].get(s, 0) >= tk[1] for o in need.values()):
                Qs[q].wait_ge(T.sem[s], tk[1])
        for tk in toks:
            for s, v in list(tk[2].items()) + [(tk[0], tk[1])]:
                if known[q].get(s, 0) < v:
                    known[q][s] = v

    def deps(q, r, w, b):
        toks = []
        for k in r:
            if k in lastw: toks.append(lastw[k])
        for k in w:
            if k in lastw: toks.append(lastw[k])
            toks.extend(readers.get(k, []))
        for k in b:
            toks.extend(tk for e, tk in bank.get(k, {}).items() if e != q)
        if q == "P":
            toks = [tk for tk in toks if tk[0] != "cP"]
        return toks

    def note(q, tok, r, w, b):
        for k in r: readers.setdefault(k, []).append(tok)
        for k in w:
            lastw[k] = tok
            readers[k] = []
        for k in b: bank.setdefault(k, {})[q] = tok

    def op(q, fn, r=(), w=(), b=(), sig=True):
        wait(q, deps(q, r, w, b))
        ins = fn()
        s = "c" + q
        if sig:
            cnt[s] += 1
            ins.then_inc(T.sem[s], 1)
            total[s] = cnt[s]
            tok = (s, cnt[s], dict(known[q]))
        else:
            tok = (s, cnt[s] + 1, dict(known[q]))
        note(q, tok, r, w, b)

    def dmas(name, items, r=(), w=()):
        s = "d_" + name
        kn = {}
        for q, out, in_ in items:
            wait(q, deps(q, r, w, ()))
            Qs[q].dma_start(out, in_).then_inc(T.sem[s], 16)
            kn = dict(known[q])
        total[s] = 16 * len(items)
        note("S", (s, total[s], kn), r, w, ())

    neng = min(len(topo.engines(a, b)) for a in cores for b in cores if a != b)

    def send(kind, sem, dst, lo, hi, r):
        wait("G", deps("G", r, (), ()))
        rid, pid, _ = topo.addr(dst)
        mask = sum(1 << e for e in topo.engines(core, dst)[:neng])
        g.remote_dma(T[kind + "R"][:, lo:hi], T[kind + "S"][:, lo:hi], T.sem[sem], T.sem.sent, pid, rid, mask)
        total["sent"] = total.get("sent", 0) + neng
        lastw[sem] = (sem, neng, {})
        total[sem] = neng

    vec, act, pe = g.vector, g.scalar, g.tensor

    def ts(out, in0, s1, s2, o0, o1, r, w, b=()):
        if o1 is None:
            op("V", lambda: vec.tensor_scalar(out, in0, s1, None, o0), r, w, b)
        else:
            op("V", lambda: vec.tensor_scalar(out, in0, s1, s2, o0, o1), r, w, b)

    def tt(out, in0, in1, o, r, w, b=()):
        op("V", lambda: vec.tensor_tensor(out, in0, in1, o), r, w, b)

    def cp(out, in_, r, w, b=()):
        op("V", lambda: vec.tensor_copy(out, in_), r, w, b)

    def ac(out, in_, f, r, w, b=(), **kw):
        op("A", lambda: act.activation(out, in_, f, **kw), r, w, b)

    def mm(out, lhsT, rhs, start, stop, r, w, b, sig=None):
        op("P", lambda: pe.matmul(out, lhsT, rhs, start, stop), r, w, b, sig=stop if sig is None else sig)

    B = [T["B%d" % i] for i in range(8)]
    pS = pG = pBM = B[4][:, 0:L]
    pU, pJ, pOL = B[4][:, L:L + 16], B[4][:, L + 16:L + 32], B[5][:, 0:16]
    pT, pCN, pF = B[6][:, 0:L], B[6][:, L:2 * L], B[7][:, 0:L]

    def load(name):
        if name == "mk": dmas("mk", [("S", T.MK[:], T.mk[:])], w=["MK"])
        if name == "xf": dmas("xf", [("S", T.XT[:, 0:W], T.xf[:])], w=["XTa"])
        if name == "st": dmas("st", [("S", T.ST[:, 0:W], T.stp[:])], w=["STa"])
        if name == "sm": dmas("sm", [("A", T.HP[:], T.hp[:]), ("A", T.CP[:], T.cp[:]), ("A", T.TH[:], T.th[:])], w=["HP", "CP", "TH"])
        if name == "xw": dmas("xw", [("S", T.XT[:, W:H], T.xf[:, 0:H - W]), ("S", T.ST[:, W:H], T.stp[:, 0:H - W])], w=["XTb", "STb"])
        if name[:2] == "pl":
            lo, hi = (0, 320) if name == "pl0" else (320, V)
            dmas(name, [("S", T.PL[:, lo:hi], T.pl[:, lo:hi])], w=["PL" + name[2]])
        if name[:2] == "su":
            h = int(name[2])
            dmas(name, [("S", T.SU[k:128:8, 640 * h:640 * h + 640], T.su[8 * h + k:128:16, :]) for k in range(8)], w=["SU%d" % h])

    for name in LOADS.split():
        load(name)

    def iota(buf, pattern, base, cm, key):
        if key == "PID":
            op("G", lambda: g.iota(buf, pattern, base, cm), (), [key])
        else:
            op("G", lambda: g.iota(buf, pattern, base, cm, allow_small_or_imprecise_dtypes=True), (), [key])

    iota(T.PID[:], [[1, 1]], 0, 1, "PID")
    iota(T.NR[:], [[1, 160]], 0, 0, "NR")
    iota(T.G16R[:], [[16, 8], [0, 16]], 0, 0, "G16R")
    iota(T.AR[:], [[0, 8], [1, 16]], 0, 0, "AR")
    iota(T.ZM[:], [[0, 256], [32, 8]], 0, 0, "ZM")

    op("V", lambda: vec.memset(T.NEG[:], -200.0), (), ["NEG"])
    op("V", lambda: vec.memset(T.ONE[:], 1.0), (), ["ONE"])
    op("V", lambda: vec.memset(T.D0[:], 0.0), (), ["D0"])
    CI, CF = T.CI, T.CF

    def ci(i): return CI[:, i:i + 1]
    def cf(i): return CF[:, i:i + 1]
    ts(ci(0), T.PID[:], 15, None, A_.bitwise_and, None, ["PID"], ["ci0"])
    ts(ci(1), T.PID[:], 1, None, A_.bitwise_and, None, ["PID"], ["ci1"])
    ts(ci(2), T.PID[:], 4, 1, A_.logical_shift_right, A_.bitwise_and, ["PID"], ["ci2"])
    ts(ci(3), T.PID[:], 112, None, A_.bitwise_and, None, ["PID"], ["ci3"])
    ts(cf(1), T.PID[:], 16.0, None, A_.add, None, ["PID"], ["cf1"])
    ts(cf(0), ci(1), -float(PK), float(PK), A_.mult, A_.add, ["ci1"], ["cf0"])
    ts(cf(2), ci(3), 16.0, None, A_.add, None, ["ci3"], ["cf2"])
    ts(cf(3), ci(3), 17.0, None, A_.add, None, ["ci3"], ["cf3"])
    ts(cf(4), ci(0), 2.0, 1.0, A_.mult, A_.add, ["ci0"], ["cf4"])
    tt(cf(5), ci(1), ci(2), A_.subtract, ["ci1", "ci2"], ["cf5"])
    ts(cf(6), ci(2), 1.0, None, A_.mult, None, ["ci2"], ["cf6"])
    ts(cf(7), ci(2), -1.0, 1.0, A_.mult, A_.add, ["ci2"], ["cf7"])
    ts(cf(8), ci(1), PK - 1.0, 1.0, A_.mult, A_.add, ["ci1"], ["cf8"])
    ts(cf(9), cf(0), -1280.0, None, A_.mult, None, ["cf0"], ["cf9"])
    ts(cf(11), ci(0), 16.0, None, A_.mult, None, ["ci0"], ["cf11"])
    ts(cf(13), ci(0), float(V), None, A_.add, None, ["ci0"], ["cf13"])
    ts(cf(14), ci(3), 1.0, None, A_.mult, None, ["ci3"], ["cf14"])
    ts(cf(15), cf(5), 15.0, cf(1), A_.mult, A_.add, ["cf5", "cf1"], ["cf15"])

    def band(buf, key, col, wt, lo=0, hi=160):
        r = ["NR", "cf%d" % col] + (["cf%d" % wt] if isinstance(wt, int) else [])
        ts(buf, T.NR[:, lo:hi], cf(col), cf(wt) if isinstance(wt, int) else wt, A_.is_equal, A_.mult, r, [key])

    def scaled(out, okey, in_, key, f):
        ac(out, in_, AF.Copy, [key], [okey], scale=f)

    band(T.ID[:], "ID", 1, 1.0, 16, 144)
    band(T.I0P[:], "I0P", 1, 7)
    band(T.I1P[:], "I1P", 1, 6)
    band(T.BP[:], "BP", 2, BIG)
    ts(T.BO1[:], T.G16R[:], cf(14), 1.0, A_.is_equal, A_.mult, ["G16R", "cf14"], ["BO1"])
    for out, key, f in ((T.IDK, "IDK", PK), (T.ID32, "ID32", 1), (T.IDM4, "IDM4", -0.25), (T.ID0, "ID0", 0), (T.ID16, "ID16", 16)):
        scaled(out[:], key, T.ID[:], "ID", float(f))
    scaled(T.I0N[:], "I0N", T.I0P[:], "I0P", -1.0)
    scaled(T.I1N[:], "I1N", T.I1P[:], "I1P", -1.0)
    scaled(T.BN[:], "BN", T.BP[:], "BP", -1.0)
    ac(T.BOP[:], T.BO1[:], AF.Sigmoid, ["BO1"], ["BOP"], bias=-128.0, scale=256.0)
    scaled(T.BON[:], "BON", T.BO1[:], "BO1", -1.0)
    ts(T.AR[:], T.AR[:], 2.0 * PAIRS, 8.0 * (PK + 1), A_.is_lt, A_.mult, ["AR"], ["AR"])
    tt(T.COR[:], T.BO1[:], T.AR[:], A_.mult, ["BO1", "AR"], ["COR"])
    band(T.WN[:], "WN", 2, 4)
    band(T.LA[:], "LA", 2, 1.0)
    band(T.LB[:], "LB", 3, 1.0)
    band(T.ID6[:], "ID6", 1, 6.0, 16, 144)
    band(T.IDH[:], "IDH", 1, 1.0, 16, 144)
    band(T.PERM[:], "PERM", 15, 1.0, 16, 144)
    tt(T.LW[:], T.LA[:], T.LB[:], A_.add, ["LA", "LB"], ["LW"])
    if PAIRS < 8:
        for out, key, f in ((T.LW1, "LW1", 1.0), (T.LWK, "LWK", float(PK))):
            ts(out[:], T.LW[:], f, None, A_.mult, None, ["LW"], [key])
    ts(T.DUM[:], T.NR[:, 0:16], 16.0, cf(13), A_.mult, A_.add, ["NR", "cf13"], ["DUM"])
    ts(T.JB[:], T.NR[:, 0:16], 256.0, cf(11), A_.mult, A_.add, ["NR", "cf11"], ["JB"])

    def targets():
        cp(T.HF[:], T.HP[:], ["HP"], ["HF"])
        ts(T.CAPB[:], T.CP[:], -127.5, -256.0, A_.add, A_.mult, ["CP"], ["CAPB"])
        ts(T.THF[:], T.TH[:], cf(8), cf(9), A_.mult, A_.add, ["TH", "cf8", "cf9"], ["THF"])
        tt(T.D1[:], T.HF[:, 16:64], T.HF[:, 0:48], A_.subtract, ["HF"], ["D1"])
        ts(T.KC[:, 3:64:4], T.HF[:, 0:16], 6.0, None, A_.mult, None, ["HF"], ["KC3"])
        tt(T.D2[:], T.D1[:, 16:48], T.D1[:, 0:32], A_.subtract, ["D1"], ["D2"])
        ts(T.KC[:, 2:64:4], T.D1[:, 0:16], 6.0, None, A_.mult, None, ["D1"], ["KC2"])
        tt(T.KC[:, 0:64:4], T.D2[:, 16:32], T.D2[:, 0:16], A_.subtract, ["D2"], ["KC0"])
        ts(T.KC[:, 1:64:4], T.D2[:, 0:16], 3.0, None, A_.mult, None, ["D2"], ["KC1"])

    mwin = T.mm[:, 0:V]
    HIGH = 9.0 / 16

    def keys(name, lo, hi, step=1): return ["%s%d" % (name, i) for i in range(lo // step, -(-hi // step))]
    def xk(lo, hi, a): return T.XK[:, 16 * lo + a:16 * hi:16]

    def gather(q, out, src, add, r, w):
        if q == "A" and add: ac(out, src, AF.Identity, r, w, bias=add)
        elif q == "A": ac(out, src, AF.Copy, r, w)
        elif add: ts(out, src, add, None, A_.add, None, r, w)
        else: cp(out, src, r, w)

    def at_least(q, out, in_, bound, r, w):
        if q == "A": ac(out, in_, AF.Sigmoid, r, w, bias=-4096.0 * (bound - 1.0 / 32), scale=4096.0)
        else: ts(out, in_, bound, None, A_.is_ge, None, r, w)

    def turn(bk, mats, mkeys, rhs, rkeys, stop, wkey):
        for h in range(2):
            for gp in range(2):
                o = 16 - 16 * (gp - h)
                last = h == 1 and gp == 1
                mm(B[bk][:, h:128:2], mats[h][:, o:o + 128], rhs(gp), False, stop and last, rkeys + mkeys, [wkey], ["B%d" % bk], sig=last)

    def step(t, name, i, q):
        d = cores[(rank + 1 + t % (n - 1)) % n]
        s_ = cores[(rank - 1 - t % (n - 1)) % n]
        first, final, cl = t == 0, t == RO - 1, t % Q
        ml, end = T.mm[:, cl:V:Q], W if first else H
        c16, c256 = slice(16 * t, 16 * t + 16), slice(L * t, L * t + L)
        half = slice(128 * i, 128 * i + 128) if i is not None else None
        if name == "levels" and q == "A": ac(mwin, T.MK[:], AF.Identity, ["MK"], ["mm"], bias=1.0 / 16, scale=1.0 / 16)
        if name == "levels" and q == "V": ts(mwin, T.MK[:], 1.0, 1.0 / 16, A_.add, A_.mult, ["MK"], ["mm"])
        if name == "places": cp(T.pp[:, 0:V], T.PL[:], ["PL0", "PL1"], ["pp"])
        if name == "targets": targets()
        if name == "own": cp(T.WF[:], T.PL[:, 0:V:Q], ["PL0", "PL1"], ["WF0", "WF1"])
        if name == "list" and first:
            lo, hi = (0, 64) if i == 0 else (64, L)
            cp(T.LST[:, lo:hi], T.PL[:, Q * lo:Q * hi:Q], ["PL%d" % i], ["LST%d" % i])
        if name == "list" and not first: cp(T.LST[:], T.pp[:, cl:V:Q], ["pp"], ["LST0", "LST1"])
        if name == "off" and i is not None: cp(T.OFF[:, half], T.SU[:, 640 * i:640 * i + 640:Q], ["SU%d" % i], ["OFF0_%d" % i])
        if name == "off" and i is None and t + 1 < Q:
            cp(T.OFF[:, L * t + L:L * t + 2 * L], T.SU[:, t + 1:V:Q], ["SU0", "SU1"], keys("OFF%d_" % (t + 1), 0, 2))
        if name in ("za", "zv"):
            h = int(name == "zv")
            c0, sl = cl * L + 128 * h + 32 * i, slice(512 * i, 512 * i + 512)
            src, r = mwin.indirect(T.OFF[:, c0:c0 + 32]), ["mm", "OFF%d_%d" % (cl, h)]
            if h: tt(T.Z[:, sl], src, T.ZA[:, sl], A_.max, r + ["ZA%d" % i], ["Z%d" % i])
            else: gather(q, T.ZA[:, sl], src, 0, r, ["ZA%d" % i])
        if name == "scan":
            op("V", lambda: vec.tensor_tensor_scan(T.Z2[:], T.ZM[:], T.Z[:], 0.0, A_.min, A_.max), ["ZM"] + keys("Z", 0, 4), ["ZS"])
        if name == "g4":
            mm(pG, T.IDM4[:], T.ONE[:], True, False, ["IDM4", "ONE"], ["G"] + keys("S", 0, 4), ["B4"])
            for l in range(2):
                mm(B[4][:, 128 * l:128 * l + 128], T.ID[:], T.Z2[:, 8 * l + 7:2048:16], False, l == 1, ["ID", "ZS"], ["G"], ["B4"])
        if name == "newa": tt(T.NEWA[:], pG, ml, A_.max, ["G", "mm"], ["NEWA"], ["B4"])
        if name == "ge8": at_least(q, T.GE8[:], ml, HIGH, ["mm"], ["GE8"])
        if name == "olg":
            mm(pOL, T.ID6[:], T.DUM[:], True, False, ["ID6", "DUM"], ["OL"], ["B5"])
            for p in range(16):
                mm(pOL, T.BP[:, 16 - p:144 - p], T.GE8[:, p:L:16], False, False, ["BP", "GE8"], ["OL"], ["B5"], sig=p == 15)
        if name == "x":
            gather(q, T.XK[:, 512 * i:512 * i + 512], T.XT[:, 0:end].indirect(T.LST[:, 32 * i:32 * i + 32]), -8.0,
                   ["XTa", "LST%d" % min(i // 2, 1)] + ([] if first else ["XTb"]), ["XK%d" % i])
        if name == "sum":
            for a in range(16):
                mm(B[4][:, 64 * i:64 * i + 64], T.ID[:], xk(64 * i, 64 * i + 64, a), a == 0, a == 15,
                   keys("XK", 2 * i, 2 * i + 2) + ["ID"], ["S%d" % i, "BM"], ["B4"])
        if name == "pack":
            lo, qs = ((0, range(8)), (128, range(4)), (128, range(4, 8)))[i]
            for p in qs:
                if p >= PAIRS: continue
                o = B[p // 2][:, (p % 2) * L + lo:(p % 2) * L + lo + 128]
                for e in range(2):
                    mm(o, (T.IDK if e else T.ID)[:], xk(lo, lo + 128, 2 * p + e), e == 0, e == 1, keys("XK", lo, lo + 128, 32) + ["ID", "IDK"],
                       ["PK%d_%d" % (p, lo // 128), ("X%d" if p & 2 else "DD%d") % (p // 4)], ["B%d" % (p // 2)])
        if name == "ov":
            ac(T.OV[:], pS, AF.Sigmoid, keys("S", 0, 4) + ["BIAS", "CAPB"], ["OV"], ["B4"], bias=(T.CAPB if first else T.BIAS)[:], scale=256.0)
        if name == "sb": ac(T.SB[:], pS, AF.Identity, keys("S", 0, 4), ["SB"], ["B4"], bias=128.0)
        if name == "pr":
            tt(T.PR[:, i * L:(i + 1) * L], B[i // 2][:, (i % 2) * L:(i % 2 + 1) * L], T.OV[:], A_.mult,
               keys("PK%d_" % i, 0, 2) + ["OV"], ["PR%d" % i], ["B%d" % (i // 2)])
        if name == "t":
            if i == 0: mm(pT, T.COR[:], T.OV[:], True, False, ["COR", "OV"], ["TT", "CN"], ["B6"])
            if i < PAIRS:
                mm(pT, T.LW[:, 16 - 2 * i:144 - 2 * i], T.PR[:, i * L:(i + 1) * L], False, i == 7, ["LW", "PR%d" % i], ["TT"], ["B6"], sig=True)
            else:
                for e in range(2):
                    c0 = 512 * (i - 6) + L * e
                    mm(pT, (T.LWK if e else T.LW1)[:, 16 - 2 * i:144 - 2 * i], T.RL[:, c0:c0 + L], False, i == 7 and e == 1,
                       ["LW1", "LWK", "RL%d" % i], ["TT"], ["B6"], sig=e == 1)
        if name == "pa":
            bk = 7 if i == 7 else 3
            for e in range(2):
                o, w = B[bk][:, L * e:L * e + L], ["PA%d" % i] + (["F15"] if i == 7 else ["X1", "PK6_0"])
                mm(o, T.ID16[:], T.OV[:], True, False, ["ID16", "OV"], w, ["B%d" % bk])
                mm(o, T.ID[:], xk(0, L, 2 * i + e), False, True, keys("XK", 0, 8) + ["ID"], w, ["B%d" % bk], sig=e == 1)
        if name == "ra":
            bk = 7 if i == 7 else 3
            ac(T.RL[:, 512 * (i - 6):512 * (i - 5)], B[bk][:], AF.Relu, ["PA%d" % i] + ([] if i == 7 else ["PK6_0"]), ["RL%d" % i], ["B%d" % bk], bias=-8.0)
        if name == "na": at_least(q, T.NA8[:], T.NEWA[:], HIGH, ["NEWA"], ["NA8"])
        if name == "hf": tt(T.HI[:], pF, T.NA8[:], A_.max, ["F15", "NA8"], ["HI"], ["B7"])
        if name == "rq" and q == "A": ac(T.RQ[:], pT, AF.Identity, ["TT"], ["RQ"], ["B6"], bias=1280.0 - 120.0 / PK, scale=1.0 / PK)
        if name == "rq" and q == "V": ts(T.RQ[:], pT, 1.0 / PK, 1280.0 - 120.0 / PK, A_.mult, A_.add, ["TT"], ["RQ"], ["B6"])
        if name == "r2": ac(T.R2[:], T.RQ[:], AF.Identity, ["RQ", "THF", "cf0"], ["R2"], bias=T.THF[:, t:t + 1], scale=cf(0))
        if name == "f": tt(pF, pT, T.R2[:], A_.is_ge, ["TT", "R2"], ["F15", "PA7"], ["B6", "B7"])
        if name == "ml": tt(ml, pF, T.NEWA[:], A_.max, ["F15", "NEWA"], ["mm"], ["B7"])
        if name == "hi": at_least(q, T.HI[:], ml, HIGH, ["mm"], ["HI"])
        if name == "pu":
            for p in range(16):
                mm(pU, T.WN[:, 16 - p:144 - p], T.SB[:, p:L:16], p == 0, p == 15, ["WN", "SB"], ["UP"], ["B4"])
        if name == "u": cp(T.U[:], pU, ["UP"], ["U"], ["B4"])
        if name == "bb": ts(T.BB[:], T.U[:], 4, 3, A_.logical_shift_right, A_.bitwise_and, ["U"], ["BB"])
        if name == "d":
            for k in range(1, 4): ts(T.D0[:, k:64:4], T.BB[:], float(k - 3), None, A_.add, None, ["BB", "D0"], ["D0%d" % k])
        if name == "c":
            op("V", lambda: vec.tensor_tensor_scan(T.C6[:], T.D0[:], T.KC[:], 0.0, A_.mult, A_.add), keys("D0", 1, 4) + keys("KC", 0, 4), ["C6"])
        if name == "cs": ts(T.cS[:, c16], T.C6[:, 3:64:4], 1.0 / 6, 0.25, A_.mult, A_.add, ["C6"], ["cS"])
        if name == "j" and i == 1: ts(T.J1[:], T.U[:], 15, None, A_.bitwise_and, None, ["U"], ["J1"])
        if name == "j" and i == 2: ts(T.J2[:], T.J1[:], 1.0, None, A_.max, None, ["J1"], ["J2"])
        if name == "pj":
            mm(pJ, T.IDH[:], T.JB[:], True, False, ["IDH", "JB"], ["JP"], ["B4"])
            mm(pJ, T.PERM[:], T.J2[:], False, True, ["PERM", "J2"], ["JP"], ["B4"])
        if name == "jl": cp(T.JL[:], pJ, ["JP"], ["JL"], ["B4"])
        if name == "ol":
            for p in range(16):
                mm(pOL, T.BN[:, 16 - p:144 - p], T.HI[:, p:L:16], False, p == 15, ["BN", "HI"], ["OL"], ["B5"])
        if name == "cn":
            mm(pCN, T.BON[:], T.GE8[:], True, False, ["BON", "GE8"], ["CN"], ["B6"])
            mm(pCN, T.BOP[:], T.HI[:], False, True, ["BOP", "HI"], ["CN"], ["B6"])
        if name == "l": tt(T.L6[:], pOL, T.C6[:, 3:64:4], A_.max, ["OL", "C6"], ["L6"], ["B5"])
        if name == "ls": ts(T.lS[:, c16], T.L6[:], 1.0 / 6, 0.25, A_.mult, A_.add, ["L6"], ["lS"])
        if name == "jk" and final: ac(T.JK[:], pCN, AF.Sigmoid, ["CN"], ["JK"], ["B6"], bias=-128.0, scale=256.0)
        if name == "jk" and not final:
            ac(T.JK[:], pCN, AF.Sigmoid, ["CN"], ["JK", "AC"], ["B6"], bias=-128.0, scale=256.0, accum_out=T.AC[:])
        if name == "ai": cp(T.AI[:], T.AC[:], ["AC"], ["AI"])
        if name == "a":
            ts(T.A7[:], T.AI[:], 7, None, A_.bitwise_and, None, ["AI"], ["A7"])
            ts(T.BIAS[:], T.A7[:], -256.0, T.CAPB[:], A_.mult, A_.add, ["A7", "CAPB"], ["BIAS"])
        if name == "s":
            gather(q, T.SK[:, 512 * i:512 * i + 512], T.ST[:, 0:end].indirect(T.LST[:, 32 * i:32 * i + 32]), 0,
                   ["STa", "LST%d" % min(i // 2, 1)] + ([] if first else ["STb"]), ["SK%d" % i])
        if name == "tr":
            sl = slice(1024 * i, 1024 * i + 1024)
            op("V", lambda: vec.transpose(T.TR[:, sl], T.SK[:, sl]), keys("SK", 2 * i, 2 * i + 2), ["TR%d" % i])
        if name == "open":
            for z in range(2):
                src, key = (T.WF[:, 128 * z:128 * z + 128], "WF%d" % z) if first else (T.pp[:, cl + 640 * z:640 * z + 640:Q], "pp")
                mm(B[2 * z][:, 0:128], T.ID0[:], T.ONE[:, 0:128], True, False, ["ID0", "ONE"],
                   ["DD%d" % z] + keys("PK%d_" % (4 * z), 0, 2) + keys("PK%d_" % (4 * z + 1), 0, 2), ["B%d" % (2 * z)])
                mm(B[2 * z + 1][:, 0:128], T.ID32[:], src, True, False, ["ID32", key],
                   ["X%d" % z] + keys("PK%d_" % (4 * z + 2), 0, 2) + keys("PK%d_" % (4 * z + 3), 0, 2), ["B%d" % (2 * z + 1)], sig=True)
        if name == "pick":
            gather("A", T.SJ[:, half], T.TR[:, 0:2048 * i + 2048].indirect(T.JL[:, 8 * i:8 * i + 8]), 0, keys("TR", 0, 2 * i + 2) + ["JL"], ["SJ%d" % i])
        if name == "turn":
            trk, move0 = keys("TR", 2 * i, 2 * i + 2), lambda gp: T.TR[:, 2048 * i + 16 * gp:2048 * i + 2048:32]
            turn(2 * i, (T.I0N, T.I1N), ["I0N", "I1N"], move0, trk, False, "DD%d" % i)
            turn(2 * i, (T.I0P, T.I1P), ["I0P", "I1P"], lambda gp: T.SJ[:, 128 * i + gp:128 * i + 128:2], ["SJ%d" % i], True, "DD%d" % i)
            turn(2 * i + 1, (T.I0P, T.I1P), ["I0P", "I1P"], move0, trk, False, "X%d" % i)
        if name == "hd": tt(T.HD[:, half], B[2 * i][:, 0:128], T.HI[:, half], A_.mult, ["DD%d" % i, "HI"], ["HD%d" % i], ["B%d" % (2 * i)])
        if name == "xs": mm(B[2 * i + 1][:, 0:128], T.ID[:], T.HD[:, half], False, True, ["ID", "HD%d" % i], ["X%d" % i], ["B%d" % (2 * i + 1)])
        if name == "ks":
            out, x, bk = T.kS[:, L * t + 128 * i:L * t + 128 * i + 128], B[2 * i + 1][:, 0:128], ["B%d" % (2 * i + 1)]
            if not final:
                cp(out, x, ["X%d" % i], ["kS%d" % i], bk)
            else:
                ts(T.WF[:, half], x, float(W), float(W), A_.is_ge, A_.mult, ["X%d" % i], ["WF%d" % i], bk)
                tt(T.WY[:, half], x, T.WF[:, half], A_.subtract, ["X%d" % i, "WF%d" % i], ["WY%d" % i], bk)
                cp(out, T.WY[:, half], ["WY%d" % i], ["kS%d" % i])
        if name == "sendc": send("c", "rc%d" % t, d, 16 * t, 16 * t + 16, ["cS"])
        if name == "sendl": send("l", "rl%d" % t, d, 16 * t, 16 * t + 16, ["lS"])
        if name == "sendb": send("b", "rb%d" % t, s_, L * t, L * t + L, ["bS"])
        if name == "sendk" and i is None: send("k", "rk%d" % t, d, L * t, L * t + L, ["kS0", "kS1"])
        if name == "sendk" and i is not None: send("k", "r%s%d" % ("kj"[i], t), d, L * t + 128 * i, L * t + 128 * i + 128, ["kS%d" % i])
        if name == "back": gather(q, T.bS[:, c256], mwin.indirect(T.cR[:, c16]), -1.25, ["mm", "rc%d" % t], ["bS"])
        if name == "zero": ac(T.mm[:].indirect(T.lR[:, c16]), T.NEG[:], AF.Sigmoid, ["NEG", "rl%d" % t], ["mm"])
        if name == "bm":
            mm(pBM, T.ID[:], T.JK[:], True, False, ["ID", "JK"], ["BM", "G"], ["B4"])
            mm(pBM, T.ID[:], T.bR[:, c256], False, True, ["ID", "rb%d" % t], ["BM"], ["B4"])
        if name == "step": tt(ml, pBM, ml, A_.max, ["BM", "mm"], ["mm"], ["B4"])
        if name in ("land", "prev"):
            u = t if name == "land" and i is not None else t - 1
            lo, w = (0, 16) if i is None else (8 * i, 8)
            cp(T.pp[:].indirect(T.lR[:, 16 * u + lo:16 * u + lo + w]), T.kR[:, L * u + 16 * lo:L * u + 16 * (lo + w)],
               ["rl%d" % u, "r%s%d" % ("kj"[i or 0], u)], ["pp"] + keys("pp", 0, 3))
        if name == "wrap":
            bk, lo, hi = ((0, 0, 512), (2, 512, 1024), (7, 1024, V))[i]
            ts(B[bk][:, 0:hi - lo], T.pp[:, lo:hi], float(W), -float(W), A_.is_ge, A_.mult, ["pp"], [("DD0", "DD1", "F15")[i]], ["B%d" % bk])
            tt(T.pp[:, lo:hi], B[bk][:, 0:hi - lo], T.pp[:, lo:hi], A_.add, [("DD0", "DD1", "F15")[i], "pp", "X0", "X1"], ["pp%d" % i], ["B%d" % bk])
        if name == "outm":
            ac(T.MK[:], mwin, AF.Relu, ["mm"], ["MK"], bias=-1.0, scale=16.0)
            dmas("ymk", [("S", T.ymk[:], T.MK[:])], r=["MK"])
        if name == "outp": dmas("ypl", [("S", T.ypl[:], T.pp[:, 0:V])], r=["pp"])

    for t in range(RO):
        for word in (FIRST if t == 0 else LAST if t == RO - 1 else MIDDLE).split():
            name, q = (word + ":").split(":")[:2]
            if name[-1].isdigit() and name != "ge8" and name != "g4" and name != "r2": step(t, name[:-1], int(name[-1]), q)
            else: step(t, name, None, q)
    for s, v in total.items():
        if known["G"].get(s, 0) < v:
            g.wait_ge(T.sem[s], v)
